import numpy as np
import ml_dtypes


def mxq(x, axis, fmt="e4m3"):
    dtype, down = {"e4m3": (ml_dtypes.float8_e4m3fn, 7), "e5m2": (ml_dtypes.float8_e5m2, 14)}[fmt]
    v = np.moveaxis(np.asarray(x, np.float32).astype(ml_dtypes.bfloat16).astype(np.float64), axis, -1)
    blocks = v.reshape(v.shape[:-1] + (-1, 32))
    amax = np.abs(blocks).max(-1, keepdims=True)
    byte = np.maximum(np.where(amax > 0, np.frexp(amax)[1] - 1 + 127, 0) - down, 1)
    scale = np.exp2(byte - 127.0)
    codes = (blocks / scale).astype(np.float32).astype(dtype).astype(np.float64)
    return np.moveaxis((codes * scale).reshape(v.shape), -1, axis)


WIDE = False


def mx_kscale(k):
    if not WIDE:
        return np.ones(k)
    levels = np.array([10, -10, 5, -5, 0])
    if k % 512:
        return np.exp2(np.random.permutation(np.resize(levels, k // 32))).repeat(32)
    a = np.empty((k // 512, 16))
    for p in range(k // 512):
        a[p, :8] = np.random.permutation(np.resize(levels, 8))
        for g in range(8):
            far = levels[np.abs(levels - a[p, g]) >= 10]
            a[p, g + 8] = far[np.random.randint(len(far))]
    return np.exp2(a.ravel()).repeat(32)


def f64(x):
    return np.asarray(x).astype(np.float64)


def striped(idx):
    return np.tile(idx.reshape(-1, 16).T, (8, 1)).astype(np.uint16)


def unstriped(offs):
    return offs[:16].T.reshape(-1).astype(np.int64)


E2M1 = np.array([0.0, 0.5, 1.0, 1.5, 2.0, 3.0, 4.0, 6.0, -0.0, -0.5, -1.0, -1.5, -2.0, -3.0, -4.0, -6.0])


def pack_weight(w, fmt):
    k, n = w.shape
    w = f64(np.asarray(w, np.float32).astype(ml_dtypes.bfloat16)).reshape(k // 32, 32, n)
    amax = np.abs(w).max(1)
    if fmt == "e4m3":
        byte = np.frexp(amax)[1] - 1 + 127 - 7
    else:
        mant, ex = np.frexp(amax / 6.0)
        byte = np.where(mant > 0.5, ex, ex - 1) + 127
    byte = np.clip(np.where(amax > 0, byte, 1), 1, 254)
    scaled = (w * np.exp2(127.0 - byte)[:, None, :]).reshape(k, n).astype(np.float32)
    by_word = np.ascontiguousarray(scaled.reshape(k // 512, 128, 4, n).transpose(0, 1, 3, 2))
    if fmt == "e4m3":
        words = by_word.astype(ml_dtypes.float8_e4m3fn).view(np.uint8)
    else:
        c = by_word.astype(ml_dtypes.float4_e2m1fn).view(np.uint8) & 0xF
        words = (c[..., 0::2] | (c[..., 1::2] << 4)).reshape(k // 512, 128, 2 * n)
    return np.ascontiguousarray(words), np.ascontiguousarray(byte.astype(np.uint8).reshape(k // 512, 16, n))


def unpack_weight(words, scales, fmt):
    g, _, n = scales.shape
    words = np.ascontiguousarray(words).reshape(g, 128, n, -1)
    if fmt == "e4m3":
        vals = words.view(ml_dtypes.float8_e4m3fn).astype(np.float64)
    else:
        nib = np.empty((g, 128, n, 4), np.uint8)
        nib[..., 0::2] = words & 0xF
        nib[..., 1::2] = words >> 4
        vals = E2M1[nib]
    vals = vals * np.repeat(np.exp2(scales.astype(np.float64) - 127.0), 8, axis=1)[..., None]
    return vals.transpose(0, 1, 3, 2).reshape(g * 512, n)


def gelu(v):
    return 0.5 * v * (1.0 + np.tanh(np.sqrt(2.0 / np.pi) * (v + 0.044715 * v**3)))


K, H, T, S, T2 = 1536, 1024, 2048, 512, 1024

def setup_inputs():
    n = np.random.standard_normal
    s = mx_kscale(K)[:, None]
    u = mx_kscale(H)[:, None]
    d = {}
    d["tab_words"], d["tab_scales"] = pack_weight(n((K, T)) * s, "e4m3")
    d["offs"] = striped(np.random.permutation(T)[:S])
    d["w1"] = (n((K, H)) / s / K ** 0.5).astype(np.float32)
    d["w2_words"], d["w2_scales"] = pack_weight(n((K, H)) / s / K ** 0.5, "e2m1")
    d["sens"] = np.exp(0.4 * n(H)).astype(np.float32)
    d["gain"] = (1.3 * np.exp(0.3 * n(H)) * u[:, 0]).astype(np.float32)
    d["wgs"] = np.exp(0.3 * n((128, S))).astype(np.float32)
    d["page0"] = (n((H, T2)) * u).astype(np.float32)
    d["offs2"] = striped(np.random.permutation(T2)[:S])
    d["offs3"] = striped(np.random.permutation(T2)[:S])
    d["shift"] = (0.6 * n(H) * u[:, 0]).astype(np.float32)
    d["w3"] = (n((H, H)) / u / H ** 0.5).astype(np.float32)
    d["back"] = (np.exp(0.3 * n(H)) / u[:, 0]).astype(np.float32)
    d["wgo"] = np.exp(0.3 * n((128, S))).astype(np.float32)
    d["page1"] = n((H, T2)).astype(np.float32)
    d["offs4"] = striped(np.random.permutation(T2)[:S])
    return d

def reference(tab_words, tab_scales, offs, w1, w2_words, w2_scales, sens, gain, wgs, page0, offs2, offs3, shift, w3, back, wgo, page1, offs4):
    v = unpack_weight(tab_words, tab_scales, "e4m3")[:, unstriped(offs)]
    a = mxq(f64(w1), 0, "e4m3").T @ v
    b = unpack_weight(w2_words, w2_scales, "e2m1").T @ v
    h = f64(gain)[:, None] * np.tanh(f64(sens)[:, None] * a + b)
    page = f64(page0).copy()
    page[:, unstriped(offs2)] = np.tile(f64(wgs), (H // 128, 1)) * h
    x = page[:, unstriped(offs3)] + f64(shift)[:, None]
    e = mxq(f64(w3), 0, "e4m3").T @ mxq(x, 0, "e4m3")
    y = np.maximum(e, f64(back)[:, None] * x)
    out = f64(page1).copy()
    out[:, unstriped(offs4)] = np.tile(f64(wgo), (H // 128, 1)) * y
    return out

@@ -1,0 +1,319 @@
+from contextlib import ExitStack
+
+import concourse.mybir as mybir
+from concourse.masks import make_identity
+
+K, H, T, S, T2 = 1536, 1024, 2048, 512, 1024
+FLOPS = 2 * S * (2 * K * H + H * H)
+
+F32 = mybir.dt.float32
+BF16 = mybir.dt.bfloat16
+I32 = mybir.dt.int32
+U32 = mybir.dt.uint32
+U16 = mybir.dt.uint16
+U8 = mybir.dt.uint8
+FP8X4 = mybir.dt.float8_e4m3fn_x4
+FP4X4 = mybir.dt.float4_e2m1fn_x4
+ALU = mybir.AluOpType
+ACT = mybir.ActivationFunctionType
+
+P = 128
+PACK = 4
+K_PASS = P * PACK
+PASSES_1 = K // K_PASS
+PASSES_2 = H // K_PASS
+SLICES = H // P
+SLICES_PER_PASS = K_PASS // P
+J_BLOCKS = S // P
+W3_WIDTH = 2 * P
+W3_UNITS = PASSES_2 * H // W3_WIDTH
+W2_FIRST = 2
+HALF = S // 2
+EARLY = 2
+RAMP = 3
+
+
+def tile_list_gassing_page_features_kernel(
+    tc, tab_words, tab_scales, offs, w1, w2_words, w2_scales, sens, gain, wgs, page0,
+    offs2, offs3, shift, w3, back, wgo, page1, offs4, out,
+):
+    nc = tc.nc
+    with ExitStack() as ctx:
+        keep = ctx.enter_context(tc.tile_pool(name="keep", bufs=1))
+        ring = ctx.enter_context(tc.tile_pool(name="ring", bufs=1))
+        psum = ctx.enter_context(tc.psum_pool(name="psum", bufs=2))
+
+        def load_list(name, source):
+            tile = keep.tile([P, S // 16], U16, name=name)
+            nc.sync.dma_start(tile[:], source)
+            return tile
+
+        def load_scale_rows(name, source, width, queue):
+            tile = keep.tile([P, PASSES_1 * width], U8, name=name, align_bytes=64)
+            nc.vector.memset(tile[:].bitcast(I32), 0)
+            for q in range(4):
+                queue.dma_start(
+                    tile[32 * q : 32 * q + 4, :].bitcast(I32).rearrange("r (a c) -> r a c", a=PASSES_1),
+                    source[:, 4 * q : 4 * q + 4, :].bitcast(I32).rearrange("a r c -> r a c"),
+                )
+            return tile
+
+        def load_tab(a):
+            tile = keep.tile([P, T], U32, name="tab%d" % a)
+            nc.sync.dma_start(tile[:].bitcast(I32), tab_words[a].rearrange("p t i -> p (t i)").bitcast(I32))
+            return tile
+
+        def load_w1(s):
+            tile = ring.tile([P, PASSES_1, PACK, P], F32, name="raw1", tag="slot%d" % s)
+            for a in range(PASSES_1):
+                rows = w1[a * K_PASS : (a + 1) * K_PASS, s * P : (s + 1) * P]
+                nc.sync.dma_start(tile[:, a, :, :], rows.rearrange("(p t) n -> p t n", t=PACK))
+            return tile
+
+        def load_w3(u):
+            c, b = divmod(u, PASSES_2)
+            tile = ring.tile([P, PACK, W3_WIDTH], F32, name="raw3", tag="slot%d" % u)
+            rows = w3[b * K_PASS : (b + 1) * K_PASS, c * W3_WIDTH : (c + 1) * W3_WIDTH]
+            nc.sync.dma_start(tile[:], rows.rearrange("(p t) n -> p t n", t=PACK))
+            return tile
+
+        def load_w2(name, lo, hi):
+            tile = keep.tile([P, PASSES_1, 2 * (hi - lo) * P], U8, name=name, align_bytes=64)
+            nc.sync.dma_start(
+                tile[:].bitcast(I32),
+                w2_words[:, :, 2 * lo * P : 2 * hi * P].bitcast(I32).rearrange("a p c -> p a c"),
+            )
+            return tile
+
+        def load_rows(name, source):
+            tile = keep.tile([P, source.shape[1]], F32, name=name)
+            nc.sync.dma_start(tile[:], source)
+            return tile
+
+        def load_p1(s):
+            tile = ring.tile([P, T2], F32, name="p1", tag="p1", bufs=4)
+            nc.sync.dma_start(tile[:], page1[s * P : (s + 1) * P, :])
+            return tile
+
+        vec_rows = keep.tile([P, P], F32, name="vec_rows")
+        nc.gpsimd.memset(vec_rows[:], 0.0)
+        for v, vec in enumerate((sens, gain, shift, back)):
+            nc.gpsimd.dma_start(vec_rows[SLICES * v : SLICES * (v + 1), :], vec.rearrange("(s p) -> s p", p=P))
+        ident = keep.tile([P, P], F32, name="ident")
+        make_identity(nc, ident[:])
+
+        raw1, raw3, p0, p1 = {}, {}, {}, {}
+        idx = load_list("idx", offs)
+        idx2 = load_list("idx2", offs2)
+        idx3 = load_list("idx3", offs3)
+        idx4 = load_list("idx4", offs4)
+        tab = [load_tab(0)]
+        tab_sc = load_scale_rows("tab_sc", tab_scales, T, nc.scalar)
+        w2_first = load_w2("w2_first", 0, W2_FIRST)
+        tab.append(load_tab(1))
+        raw1[0] = load_w1(0)
+        tab.append(load_tab(2))
+        w2_sc = load_scale_rows("w2_sc", w2_scales, H, nc.sync)
+        raw1[1] = load_w1(1)
+        wgs_sb = load_rows("wgs_sb", wgs)
+        p0[0] = load_rows("p0_0", page0[0:P, :])
+        raw1[2] = load_w1(2)
+        w2_rest = load_w2("w2_rest", W2_FIRST, SLICES)
+        for s in range(1, SLICES):
+            p0[s] = load_rows("p0_%d" % s, page0[s * P : (s + 1) * P, :])
+            if s + 2 < SLICES:
+                raw1[s + 2] = load_w1(s + 2)
+        wgo_sb = load_rows("wgo_sb", wgo)
+
+        v_words = keep.tile([P, PASSES_1, S], U32, name="v_words", align_bytes=64)
+        v_sc = keep.tile([P, PASSES_1, S], U8, name="v_sc", align_bytes=64)
+        for a in range(PASSES_1):
+            nc.vector.tensor_copy(v_sc[:, a, :], tab_sc[:, a * T : (a + 1) * T].indirect(idx[:]))
+        for a in range(PASSES_1):
+            nc.vector.tensor_copy(v_words[:, a, :], tab[a][:].indirect(idx[:]))
+
+        vec_ps = psum.tile([P, P], F32, name="vec_ps", tag="turn")
+        nc.tensor.transpose(vec_ps[:], vec_rows[:], ident[:])
+        vec_cols = keep.tile([P, 4 * SLICES], F32, name="vec_cols")
+        nc.scalar.copy(vec_cols[:], vec_ps[:, 0 : 4 * SLICES])
+
+        def column(v, s):
+            return vec_cols[:, SLICES * v + s : SLICES * v + s + 1]
+
+        w1q, w3q, woven3 = {}, {}, {}
+        gw, th, y = {}, {}, {}
+        work = [keep.tile([P, S + HALF], F32, name="work%d" % s) for s in range(SLICES + 2)]
+        z = [work[s][:, 0:S] for s in range(SLICES)]
+        picked_early = [work[s + 1][:, 0:HALF] for s in range(SLICES)]
+        x = [work[s + 2][:, HALF : HALF + S] for s in range(SLICES)]
+        x_turned = {}
+        x_codes = [keep.tile([P, S], U32, name="x_codes%d" % b, align_bytes=64) for b in range(PASSES_2)]
+        x_scales = [keep.tile([P, S], U8, name="x_scales%d" % b, align_bytes=64) for b in range(PASSES_2)]
+
+        def quantise_w1(s):
+            codes = ring.tile([P, PASSES_1 * P], U32, name="w1_codes", tag="w1_codes", bufs=3, align_bytes=64)
+            scales = ring.tile([P, PASSES_1 * P], U8, name="w1_scales", tag="w1_scales", bufs=3, align_bytes=64)
+            woven = ring.tile([P, PASSES_1 * K_PASS], BF16, name="woven", tag="woven", bufs=3, align_bytes=64)
+            for lo, hi in ((0, 2), (2, 3)):
+                part = woven[:, lo * K_PASS : hi * K_PASS]
+                nc.scalar.copy(
+                    part.rearrange("p (a c i t) -> p a c t i", a=hi - lo, i=4, t=PACK),
+                    raw1[s][:, lo:hi, :, :].rearrange("p a t (c i) -> p a c t i", i=4),
+                )
+                cols = slice(lo * P, hi * P)
+                nc.vector.quantize_mx(out=codes[:, cols].bitcast(FP8X4), scales=scales[:, cols], in_=part)
+            w1q[s] = codes, scales
+
+        def weave_w3(u):
+            woven3[u] = ring.tile([P, W3_WIDTH * PACK], BF16, name="woven3", tag="woven", bufs=3, align_bytes=64)
+            nc.scalar.copy(
+                woven3[u][:].rearrange("p (c i t) -> p c t i", i=4, t=PACK),
+                raw3[u][:].rearrange("p t (c i) -> p c t i", i=4),
+            )
+
+        def quantise_w3(u):
+            codes = keep.tile([P, W3_WIDTH], U32, name="w3_codes%d" % u, align_bytes=64)
+            scales = keep.tile([P, W3_WIDTH], U8, name="w3_scales%d" % u, align_bytes=64)
+            nc.vector.quantize_mx(out=codes[:].bitcast(FP8X4), scales=scales[:], in_=woven3[u][:])
+            w3q[u] = codes, scales
+
+        def first_products(s):
+            a_ps = psum.tile([P, S], F32, name="a_ps", tag="sum_a")
+            b_ps = psum.tile([P, S], F32, name="b_ps", tag="sum_b")
+            w2_tile, w2_col = (w2_first, s) if s < W2_FIRST else (w2_rest, s - W2_FIRST)
+            codes, scales = w1q[s]
+            for a in range(PASSES_1):
+                flags = dict(start=(a == 0), stop=(a == PASSES_1 - 1))
+                moving = dict(rhs=v_words[:, a, :].bitcast(FP8X4), rhs_scale=v_sc[:, a, :])
+                nc.tensor.matmul_mx(
+                    out=b_ps[:],
+                    lhsT=w2_tile[:, a, 2 * P * w2_col : 2 * P * (w2_col + 1)].bitcast(FP4X4),
+                    lhsT_scale=w2_sc[:, a * H + s * P : a * H + (s + 1) * P],
+                    **moving, **flags,
+                )
+                cols = slice(a * P, (a + 1) * P)
+                nc.tensor.matmul_mx(
+                    out=a_ps[:], lhsT=codes[:, cols].bitcast(FP8X4), lhsT_scale=scales[:, cols], **moving, **flags
+                )
+            nc.scalar.copy(z[s], b_ps[:])
+            nc.vector.scalar_tensor_tensor(z[s], a_ps[:], column(0, s), z[s], ALU.mult, ALU.add)
+
+        def anchor(s):
+            return s + 2 if s >= RAMP else s + min(s, 1)
+
+        def put_state(s):
+            if s < SLICES - 1:
+                gw[s] = ring.tile([P, S], F32, name="gw", tag="gw", bufs=2)
+            else:
+                gw[s] = ring.tile([P, S], F32, name="gw_last", tag="late")
+            nc.scalar.activation(gw[s][:], wgs_sb[:], ACT.Copy, scale=column(1, s))
+            th[s] = ring.tile([P, S], F32, name="th", tag="slot%d" % anchor(s))
+            nc.scalar.activation(th[s][:], z[s], ACT.Tanh)
+            nc.vector.tensor_tensor(p0[s][:].indirect(idx2[:]), th[s][:], gw[s][:], ALU.mult)
+
+        def list_half(offsets, half):
+            return offsets[:, half * HALF // 16 : (half + 1) * HALF // 16]
+
+        def recall(s, half, picked):
+            nc.vector.tensor_copy(picked, p0[s][:].indirect(list_half(idx3, half)))
+
+        def turn(s, half, picked):
+            b, q = divmod(s, SLICES_PER_PASS)
+            x_half = x[s][:, half * HALF : (half + 1) * HALF]
+            nc.scalar.activation(x_half, picked, ACT.Identity, bias=column(2, s))
+            turned_ps = psum.tile([P, 2, P], F32, name="turned_ps", tag="turn")
+            for c in range(2):
+                nc.tensor.transpose(turned_ps[:, c, :], x_half[:, c * P : (c + 1) * P], ident[:])
+            if q == 0:
+                x_turned[half, b] = keep.tile([P, 2, 2, SLICES_PER_PASS, 32, 2], BF16, name="x_turned%d%d" % (half, b))
+            nc.scalar.copy(
+                x_turned[half, b][:, :, :, q, :, :],
+                turned_ps[:].rearrange("j c (m u e) -> j c u m e", u=2, e=2),
+            )
+            if q == SLICES_PER_PASS - 1:
+                quantise_x(half, b)
+
+        def quantise_x(half, b):
+            words = x_turned[half, b][:].rearrange("j c u q m e -> j (c u q m e)").bitcast(F32)
+            tag = "late2" if (half, b) == (0, PASSES_2 - 1) else "x_woven"
+            woven = ring.tile([P, HALF * PACK], BF16, name="x_woven", tag=tag, align_bytes=64)
+            back_ps = psum.tile([P, 2, 2, P], F32, name="back_ps", tag="turn_back")
+            for c in range(2):
+                for u in range(2):
+                    first = (c * 2 + u) * P
+                    nc.tensor.transpose(back_ps[:, c, u, :], words[:, first : first + P], ident[:])
+            nc.scalar.copy(
+                woven[:].bitcast(F32).rearrange("p (c j u) -> p c j u", c=2, u=2),
+                back_ps[:].rearrange("p c u j -> p c j u"),
+            )
+            cols = slice(half * HALF, (half + 1) * HALF)
+            nc.vector.quantize_mx(out=x_codes[b][:, cols].bitcast(FP8X4), scales=x_scales[b][:, cols], in_=woven[:])
+
+        def second_stage(s, lo, hi, result):
+            e_ps = psum.tile([P, hi - lo], F32, name="e_ps", tag=("sum_a", "sum_b")[s % 2])
+            for b in reversed(range(PASSES_2)):
+                codes, scales = w3q[PASSES_2 * (s // 2) + b]
+                cols = slice((s % 2) * P, (s % 2 + 1) * P)
+                nc.tensor.matmul_mx(
+                    out=e_ps[:], lhsT=codes[:, cols].bitcast(FP8X4), lhsT_scale=scales[:, cols],
+                    rhs=x_codes[b][:, lo:hi].bitcast(FP8X4), rhs_scale=x_scales[b][:, lo:hi],
+                    start=(b == PASSES_2 - 1), stop=(b == 0),
+                )
+            nc.vector.scalar_tensor_tensor(result, x[s][:, lo:hi], column(3, s), e_ps[:], ALU.mult, ALU.max)
+
+        def put_features(s, lo, hi, values):
+            offsets = idx4[:, lo // 16 : hi // 16]
+            nc.vector.tensor_tensor(p1[s][:].indirect(offsets), values, wgo_sb[:, lo:hi], ALU.mult)
+            if hi == S:
+                nc.sync.dma_start(out[s * P : (s + 1) * P, :], p1[s][:])
+
+        quantise_w1(0)
+        first_products(0)
+        quantise_w1(1)
+        for s in range(SLICES):
+            for ahead in range(anchor(s - 1) + 1, anchor(s) + 1):
+                if 1 < ahead < SLICES:
+                    quantise_w1(ahead)
+            if RAMP <= s < SLICES - 1:
+                first_products(s + 1)
+            put_state(s)
+            if s < RAMP:
+                first_products(s + 1)
+            if s > 0:
+                recall(s - 1, 0, picked_early[s - 1])
+            if s > 1:
+                turn(s - 2, 0, picked_early[s - 2])
+            raw3[s] = load_w3(s)
+            if s < 4:
+                p1[s] = load_p1(s)
+            for u in range(W3_UNITS):
+                if s == SLICES - 3 + (u + 1) // 3:
+                    weave_w3(u)
+                    quantise_w3(u)
+        recall(SLICES - 1, 0, picked_early[SLICES - 1])
+        for s in (SLICES - 2, SLICES - 1):
+            turn(s, 0, picked_early[s])
+        for s in range(EARLY):
+            second_stage(s, 0, HALF, x[s][:, 0:HALF])
+        picked_late = [
+            ring.tile([P, SLICES_PER_PASS, HALF], F32, name="picked_late0", tag="late"),
+            ring.tile([P, SLICES_PER_PASS, HALF], F32, name="picked_late1", tag="late2", align_bytes=64),
+        ]
+        for s in range(SLICES):
+            b, q = divmod(s, SLICES_PER_PASS)
+            recall(s, 1, picked_late[b][:, q, :])
+            turn(s, 1, picked_late[b][:, q, :])
+        for s in range(EARLY):
+            put_features(s, 0, HALF, x[s][:, 0:HALF])
+
+        def start_second(s):
+            lo = HALF if s < EARLY else 0
+            second_stage(s, lo, S, x[s][:, lo:S])
+
+        start_second(0)
+        for s in range(SLICES):
+            if s + 1 < SLICES:
+                start_second(s + 1)
+            put_features(s, HALF if s < EARLY else 0, S, x[s][:, HALF if s < EARLY else 0 : S])
+            if s + 4 < SLICES:
+                p1[s + 4] = load_p1(s + 4)

@@ -29,7 +29,8 @@ W3_WIDTH = 2 * P
 W3_UNITS = PASSES_2 * H // W3_WIDTH
 W2_FIRST = 2
 HALF = S // 2
-EARLY = 2
+EARLY = 3
+LATE_SPLIT = 6
 RAMP = 3
 
 
@@ -48,20 +49,23 @@ def tile_list_gassing_page_features_kernel(
             nc.sync.dma_start(tile[:], source)
             return tile
 
-        def load_scale_rows(name, source, width, queue):
+        def load_scale_rows(name, source, width, clearer):
             tile = keep.tile([P, PASSES_1 * width], U8, name=name, align_bytes=64)
-            nc.vector.memset(tile[:].bitcast(I32), 0)
+            clearer.memset(tile[:].bitcast(I32), 0)
             for q in range(4):
-                queue.dma_start(
+                nc.scalar.dma_start(
                     tile[32 * q : 32 * q + 4, :].bitcast(I32).rearrange("r (a c) -> r a c", a=PASSES_1),
                     source[:, 4 * q : 4 * q + 4, :].bitcast(I32).rearrange("a r c -> r a c"),
                 )
             return tile
 
-        def load_tab(a):
-            tile = keep.tile([P, T], U32, name="tab%d" % a)
-            nc.sync.dma_start(tile[:].bitcast(I32), tab_words[a].rearrange("p t i -> p (t i)").bitcast(I32))
-            return tile
+        def load_tab(lo, hi):
+            tile = keep.tile([P, (hi - lo) * T], U32, name="tab%d" % lo)
+            nc.sync.dma_start(
+                tile[:].bitcast(I32).rearrange("p (a t) -> p a t", a=hi - lo),
+                tab_words[lo:hi].rearrange("a p t i -> p a (t i)").bitcast(I32),
+            )
+            return [tile[:, a * T : (a + 1) * T] for a in range(hi - lo)]
 
         def load_w1(s):
             tile = ring.tile([P, PASSES_1, PACK, P], F32, name="raw1", tag="slot%d" % s)
@@ -91,46 +95,43 @@ def tile_list_gassing_page_features_kernel(
             return tile
 
         def load_p1(s):
-            tile = ring.tile([P, T2], F32, name="p1", tag="p1", bufs=4)
+            tile = ring.tile([P, T2], F32, name="p1", tag="p1_%d" % s if s < 4 else "slot%d" % (0, 2, 4, 5)[s - 4])
             nc.sync.dma_start(tile[:], page1[s * P : (s + 1) * P, :])
             return tile
 
+        raw1, raw3, p0, p1 = {}, {}, {}, {}
+        idx = load_list("idx", offs)
+        tab = load_tab(0, 1)
+        tab_sc = load_scale_rows("tab_sc", tab_scales, T, nc.vector)
         vec_rows = keep.tile([P, P], F32, name="vec_rows")
         nc.gpsimd.memset(vec_rows[:], 0.0)
         for v, vec in enumerate((sens, gain, shift, back)):
             nc.gpsimd.dma_start(vec_rows[SLICES * v : SLICES * (v + 1), :], vec.rearrange("(s p) -> s p", p=P))
         ident = keep.tile([P, P], F32, name="ident")
         make_identity(nc, ident[:])
-
-        raw1, raw3, p0, p1 = {}, {}, {}, {}
-        idx = load_list("idx", offs)
-        idx2 = load_list("idx2", offs2)
-        idx3 = load_list("idx3", offs3)
-        idx4 = load_list("idx4", offs4)
-        tab = [load_tab(0)]
-        tab_sc = load_scale_rows("tab_sc", tab_scales, T, nc.scalar)
-        w2_first = load_w2("w2_first", 0, W2_FIRST)
-        tab.append(load_tab(1))
-        raw1[0] = load_w1(0)
-        tab.append(load_tab(2))
-        w2_sc = load_scale_rows("w2_sc", w2_scales, H, nc.sync)
-        raw1[1] = load_w1(1)
+        w2_sc = load_scale_rows("w2_sc", w2_scales, H, nc.gpsimd)
+        warm = keep.tile([P, 1], F32, name="warm")
+        nc.scalar.activation(warm[:], ident[:, 0:1], ACT.Tanh)
         wgs_sb = load_rows("wgs_sb", wgs)
+        tab = tab + load_tab(1, 2) + load_tab(2, 3)
+        w2_first = load_w2("w2_first", 0, W2_FIRST)
+        raw1[0] = load_w1(0)
+        raw1[1] = load_w1(1)
+        idx2 = load_list("idx2", offs2)
         p0[0] = load_rows("p0_0", page0[0:P, :])
-        raw1[2] = load_w1(2)
         w2_rest = load_w2("w2_rest", W2_FIRST, SLICES)
-        for s in range(1, SLICES):
+        raw1[2] = load_w1(2)
+        idx3 = load_list("idx3", offs3)
+        for s in range(1, SLICES - 2):
             p0[s] = load_rows("p0_%d" % s, page0[s * P : (s + 1) * P, :])
-            if s + 2 < SLICES:
-                raw1[s + 2] = load_w1(s + 2)
-        wgo_sb = load_rows("wgo_sb", wgo)
+            raw1[s + 2] = load_w1(s + 2)
 
         v_words = keep.tile([P, PASSES_1, S], U32, name="v_words", align_bytes=64)
         v_sc = keep.tile([P, PASSES_1, S], U8, name="v_sc", align_bytes=64)
         for a in range(PASSES_1):
             nc.vector.tensor_copy(v_sc[:, a, :], tab_sc[:, a * T : (a + 1) * T].indirect(idx[:]))
         for a in range(PASSES_1):
-            nc.vector.tensor_copy(v_words[:, a, :], tab[a][:].indirect(idx[:]))
+            nc.vector.tensor_copy(v_words[:, a, :], tab[a].indirect(idx[:]))
 
         vec_ps = psum.tile([P, P], F32, name="vec_ps", tag="turn")
         nc.tensor.transpose(vec_ps[:], vec_rows[:], ident[:])
@@ -141,9 +142,12 @@ def tile_list_gassing_page_features_kernel(
             return vec_cols[:, SLICES * v + s : SLICES * v + s + 1]
 
         w1q, w3q, woven3 = {}, {}, {}
-        gw, th, y = {}, {}, {}
+        stage = {}
         work = [keep.tile([P, S + HALF], F32, name="work%d" % s) for s in range(SLICES + 2)]
         z = [work[s][:, 0:S] for s in range(SLICES)]
+        gw = [work[s + 2 if s > RAMP else s + 1][:, 0:S] for s in range(SLICES)]
+        for s in range(SLICES):
+            nc.scalar.activation(gw[s], wgs_sb[:], ACT.Copy, scale=column(1, s))
         picked_early = [work[s + 1][:, 0:HALF] for s in range(SLICES)]
         x = [work[s + 2][:, HALF : HALF + S] for s in range(SLICES)]
         x_turned = {}
@@ -154,7 +158,7 @@ def tile_list_gassing_page_features_kernel(
             codes = ring.tile([P, PASSES_1 * P], U32, name="w1_codes", tag="w1_codes", bufs=3, align_bytes=64)
             scales = ring.tile([P, PASSES_1 * P], U8, name="w1_scales", tag="w1_scales", bufs=3, align_bytes=64)
             woven = ring.tile([P, PASSES_1 * K_PASS], BF16, name="woven", tag="woven", bufs=3, align_bytes=64)
-            for lo, hi in ((0, 2), (2, 3)):
+            for lo, hi in ((0, 1), (1, 2), (2, 3)) if s < 2 else ((0, 2), (2, 3)):
                 part = woven[:, lo * K_PASS : hi * K_PASS]
                 nc.scalar.copy(
                     part.rearrange("p (a c i t) -> p a c t i", a=hi - lo, i=4, t=PACK),
@@ -165,7 +169,11 @@ def tile_list_gassing_page_features_kernel(
             w1q[s] = codes, scales
 
         def weave_w3(u):
-            woven3[u] = ring.tile([P, W3_WIDTH * PACK], BF16, name="woven3", tag="woven", bufs=3, align_bytes=64)
+            if u < 4:
+                woven3[u] = ring.tile([P, W3_WIDTH * PACK], BF16, name="woven3", tag="woven", bufs=3, align_bytes=64)
+            else:
+                tag = ("x_turned11", "x_woven")[u % 2]
+                woven3[u] = ring.tile([P, W3_WIDTH * PACK], BF16, name="woven3", tag=tag, align_bytes=64)
             nc.scalar.copy(
                 woven3[u][:].rearrange("p (c i t) -> p c t i", i=4, t=PACK),
                 raw3[u][:].rearrange("p t (c i) -> p c t i", i=4),
@@ -195,21 +203,23 @@ def tile_list_gassing_page_features_kernel(
                 nc.tensor.matmul_mx(
                     out=a_ps[:], lhsT=codes[:, cols].bitcast(FP8X4), lhsT_scale=scales[:, cols], **moving, **flags
                 )
-            nc.scalar.copy(z[s], b_ps[:])
-            nc.vector.scalar_tensor_tensor(z[s], a_ps[:], column(0, s), z[s], ALU.mult, ALU.add)
+            b_sb = staged(s)[:, 0, :] if s > 0 else z[s]
+            nc.scalar.copy(b_sb, b_ps[:])
+            nc.vector.scalar_tensor_tensor(z[s], a_ps[:], column(0, s), b_sb, ALU.mult, ALU.add)
 
         def anchor(s):
-            return s + 2 if s >= RAMP else s + min(s, 1)
+            return s + 2 if s >= RAMP else s + 1
+
+        def staged(n):
+            if n not in stage:
+                slot = n if n < SLICES else 2 * (n - SLICES) + 1
+                stage[n] = ring.tile([P, 2, S], F32, name="stage", tag="slot%d" % slot)
+            return stage[n]
 
         def put_state(s):
-            if s < SLICES - 1:
-                gw[s] = ring.tile([P, S], F32, name="gw", tag="gw", bufs=2)
-            else:
-                gw[s] = ring.tile([P, S], F32, name="gw_last", tag="late")
-            nc.scalar.activation(gw[s][:], wgs_sb[:], ACT.Copy, scale=column(1, s))
-            th[s] = ring.tile([P, S], F32, name="th", tag="slot%d" % anchor(s))
-            nc.scalar.activation(th[s][:], z[s], ACT.Tanh)
-            nc.vector.tensor_tensor(p0[s][:].indirect(idx2[:]), th[s][:], gw[s][:], ALU.mult)
+            th = staged(anchor(s))[:, 1, :]
+            nc.scalar.activation(th, z[s], ACT.Tanh)
+            nc.vector.tensor_tensor(p0[s][:].indirect(idx2[:]), th, gw[s], ALU.mult)
 
         def list_half(offsets, half):
             return offsets[:, half * HALF // 16 : (half + 1) * HALF // 16]
@@ -225,7 +235,9 @@ def tile_list_gassing_page_features_kernel(
             for c in range(2):
                 nc.tensor.transpose(turned_ps[:, c, :], x_half[:, c * P : (c + 1) * P], ident[:])
             if q == 0:
-                x_turned[half, b] = keep.tile([P, 2, 2, SLICES_PER_PASS, 32, 2], BF16, name="x_turned%d%d" % (half, b))
+                x_turned[half, b] = ring.tile(
+                    [P, 2, 2, SLICES_PER_PASS, 32, 2], BF16, name="x_turned%d%d" % (half, b), align_bytes=64
+                )
             nc.scalar.copy(
                 x_turned[half, b][:, :, :, q, :, :],
                 turned_ps[:].rearrange("j c (m u e) -> j c u m e", u=2, e=2),
@@ -235,7 +247,7 @@ def tile_list_gassing_page_features_kernel(
 
         def quantise_x(half, b):
             words = x_turned[half, b][:].rearrange("j c u q m e -> j (c u q m e)").bitcast(F32)
-            tag = "late2" if (half, b) == (0, PASSES_2 - 1) else "x_woven"
+            tag = "x_woven_first" if b == 0 else ("late2", "x_woven")[half]
             woven = ring.tile([P, HALF * PACK], BF16, name="x_woven", tag=tag, align_bytes=64)
             back_ps = psum.tile([P, 2, 2, P], F32, name="back_ps", tag="turn_back")
             for c in range(2):
@@ -267,44 +279,59 @@ def tile_list_gassing_page_features_kernel(
             if hi == S:
                 nc.sync.dma_start(out[s * P : (s + 1) * P, :], p1[s][:])
 
+        def prepare_w3(u):
+            raw3[u] = load_w3(u)
+            weave_w3(u)
+            quantise_w3(u)
+
         quantise_w1(0)
         first_products(0)
-        quantise_w1(1)
+        done = 0
         for s in range(SLICES):
             for ahead in range(anchor(s - 1) + 1, anchor(s) + 1):
-                if 1 < ahead < SLICES:
+                if ahead < SLICES:
                     quantise_w1(ahead)
-            if RAMP <= s < SLICES - 1:
-                first_products(s + 1)
+                else:
+                    prepare_w3(2 * (ahead - SLICES))
+                    prepare_w3(2 * (ahead - SLICES) + 1)
+                    p0[s] = load_rows("p0_%d" % s, page0[s * P : (s + 1) * P, :])
             put_state(s)
-            if s < RAMP:
-                first_products(s + 1)
             if s > 0:
                 recall(s - 1, 0, picked_early[s - 1])
+            for ahead in range(done + 1, min(anchor(s), SLICES - 1) + 1):
+                first_products(ahead)
+                done = ahead
             if s > 1:
                 turn(s - 2, 0, picked_early[s - 2])
-            raw3[s] = load_w3(s)
-            if s < 4:
-                p1[s] = load_p1(s)
-            for u in range(W3_UNITS):
-                if s == SLICES - 3 + (u + 1) // 3:
-                    weave_w3(u)
-                    quantise_w3(u)
+        wgo_sb = load_rows("wgo_sb", wgo)
+        idx4 = load_list("idx4", offs4)
+        for s in range(EARLY):
+            p1[s] = load_p1(s)
+        for u in range(4, W3_UNITS):
+            raw3[u] = load_w3(u)
+        for s in range(EARLY, SLICES - 2):
+            p1[s] = load_p1(s)
         recall(SLICES - 1, 0, picked_early[SLICES - 1])
         for s in (SLICES - 2, SLICES - 1):
             turn(s, 0, picked_early[s])
-        for s in range(EARLY):
+        for s in range(EARLY - 1):
             second_stage(s, 0, HALF, x[s][:, 0:HALF])
-        picked_late = [
-            ring.tile([P, SLICES_PER_PASS, HALF], F32, name="picked_late0", tag="late"),
-            ring.tile([P, SLICES_PER_PASS, HALF], F32, name="picked_late1", tag="late2", align_bytes=64),
-        ]
+        late0 = ring.tile([P, LATE_SPLIT, HALF], F32, name="picked_late0", tag="slot3")
+        late1 = ring.tile([P, SLICES - LATE_SPLIT, HALF], F32, name="picked_late1", tag="late2", align_bytes=64)
         for s in range(SLICES):
-            b, q = divmod(s, SLICES_PER_PASS)
-            recall(s, 1, picked_late[b][:, q, :])
-            turn(s, 1, picked_late[b][:, q, :])
-        for s in range(EARLY):
+            picked = late0[:, s, :] if s < LATE_SPLIT else late1[:, s - LATE_SPLIT, :]
+            recall(s, 1, picked)
+            turn(s, 1, picked)
+        for s in range(EARLY - 1):
             put_features(s, 0, HALF, x[s][:, 0:HALF])
+        filler = ring.tile([P, HALF], F32, name="y_early", tag="x_woven", align_bytes=64)
+        second_stage(EARLY - 1, 0, HALF, filler[:])
+        put_features(EARLY - 1, 0, HALF, filler[:])
+        for u in range(4, W3_UNITS):
+            weave_w3(u)
+            quantise_w3(u)
+        for s in range(SLICES - 2, SLICES):
+            p1[s] = load_p1(s)
 
         def start_second(s):
             lo = HALF if s < EARLY else 0
@@ -314,6 +341,5 @@ def tile_list_gassing_page_features_kernel(
         for s in range(SLICES):
             if s + 1 < SLICES:
                 start_second(s + 1)
-            put_features(s, HALF if s < EARLY else 0, S, x[s][:, HALF if s < EARLY else 0 : S])
-            if s + 4 < SLICES:
-                p1[s + 4] = load_p1(s + 4)
+            lo = HALF if s < EARLY else 0
+            put_features(s, lo, S, x[s][:, lo:S])

@@ -27,11 +27,11 @@ SLICES_PER_PASS = K_PASS // P
 J_BLOCKS = S // P
 W3_WIDTH = 2 * P
 W3_UNITS = PASSES_2 * H // W3_WIDTH
-W2_FIRST = 2
+W2_PARTS = ((0, 2), (2, 4), (4, 8))
 HALF = S // 2
 EARLY = 3
 LATE_SPLIT = 6
-RAMP = 3
+RAMP = 4
 
 
 def tile_list_gassing_page_features_kernel(
@@ -49,11 +49,11 @@ def tile_list_gassing_page_features_kernel(
             nc.sync.dma_start(tile[:], source)
             return tile
 
-        def load_scale_rows(name, source, width, clearer):
+        def load_scale_rows(name, source, width, queue):
             tile = keep.tile([P, PASSES_1 * width], U8, name=name, align_bytes=64)
-            clearer.memset(tile[:].bitcast(I32), 0)
+            nc.vector.memset(tile[:].bitcast(I32), 0)
             for q in range(4):
-                nc.scalar.dma_start(
+                queue.dma_start(
                     tile[32 * q : 32 * q + 4, :].bitcast(I32).rearrange("r (a c) -> r a c", a=PASSES_1),
                     source[:, 4 * q : 4 * q + 4, :].bitcast(I32).rearrange("a r c -> r a c"),
                 )
@@ -81,8 +81,8 @@ def tile_list_gassing_page_features_kernel(
             nc.sync.dma_start(tile[:], rows.rearrange("(p t) n -> p t n", t=PACK))
             return tile
 
-        def load_w2(name, lo, hi):
-            tile = keep.tile([P, PASSES_1, 2 * (hi - lo) * P], U8, name=name, align_bytes=64)
+        def load_w2(lo, hi):
+            tile = keep.tile([P, PASSES_1, 2 * (hi - lo) * P], U8, name="w2_%d" % lo, align_bytes=64)
             nc.sync.dma_start(
                 tile[:].bitcast(I32),
                 w2_words[:, :, 2 * lo * P : 2 * hi * P].bitcast(I32).rearrange("a p c -> p a c"),
@@ -101,29 +101,29 @@ def tile_list_gassing_page_features_kernel(
 
         raw1, raw3, p0, p1 = {}, {}, {}, {}
         idx = load_list("idx", offs)
+        wgs_sb = load_rows("wgs_sb", wgs)
         tab = load_tab(0, 1)
-        tab_sc = load_scale_rows("tab_sc", tab_scales, T, nc.vector)
         vec_rows = keep.tile([P, P], F32, name="vec_rows")
         nc.gpsimd.memset(vec_rows[:], 0.0)
         for v, vec in enumerate((sens, gain, shift, back)):
-            nc.gpsimd.dma_start(vec_rows[SLICES * v : SLICES * (v + 1), :], vec.rearrange("(s p) -> s p", p=P))
+            nc.scalar.dma_start(vec_rows[SLICES * v : SLICES * (v + 1), :], vec.rearrange("(s p) -> s p", p=P))
         ident = keep.tile([P, P], F32, name="ident")
         make_identity(nc, ident[:])
-        w2_sc = load_scale_rows("w2_sc", w2_scales, H, nc.gpsimd)
-        warm = keep.tile([P, 1], F32, name="warm")
-        nc.scalar.activation(warm[:], ident[:, 0:1], ACT.Tanh)
-        wgs_sb = load_rows("wgs_sb", wgs)
+        tab_sc = load_scale_rows("tab_sc", tab_scales, T, nc.scalar)
         tab = tab + load_tab(1, 2) + load_tab(2, 3)
-        w2_first = load_w2("w2_first", 0, W2_FIRST)
+        w2_sc = load_scale_rows("w2_sc", w2_scales, H, nc.sync)
+        w2_parts = [load_w2(*W2_PARTS[0])]
         raw1[0] = load_w1(0)
         raw1[1] = load_w1(1)
         idx2 = load_list("idx2", offs2)
         p0[0] = load_rows("p0_0", page0[0:P, :])
-        w2_rest = load_w2("w2_rest", W2_FIRST, SLICES)
+        w2_parts.append(load_w2(*W2_PARTS[1]))
         raw1[2] = load_w1(2)
         idx3 = load_list("idx3", offs3)
         for s in range(1, SLICES - 2):
             p0[s] = load_rows("p0_%d" % s, page0[s * P : (s + 1) * P, :])
+            if s + 2 == W2_PARTS[2][0]:
+                w2_parts.append(load_w2(*W2_PARTS[2]))
             raw1[s + 2] = load_w1(s + 2)
 
         v_words = keep.tile([P, PASSES_1, S], U32, name="v_words", align_bytes=64)
@@ -160,9 +160,10 @@ def tile_list_gassing_page_features_kernel(
             woven = ring.tile([P, PASSES_1 * K_PASS], BF16, name="woven", tag="woven", bufs=3, align_bytes=64)
             for lo, hi in ((0, 1), (1, 2), (2, 3)) if s < 2 else ((0, 2), (2, 3)):
                 part = woven[:, lo * K_PASS : hi * K_PASS]
-                nc.scalar.copy(
-                    part.rearrange("p (a c i t) -> p a c t i", a=hi - lo, i=4, t=PACK),
-                    raw1[s][:, lo:hi, :, :].rearrange("p a t (c i) -> p a c t i", i=4),
+                weave = nc.vector.tensor_copy if s < 2 else nc.scalar.copy
+                weave(
+                    part.rearrange("p (a n t) -> p a n t", a=hi - lo, t=PACK),
+                    raw1[s][:, lo:hi, :, :].rearrange("p a t n -> p a n t"),
                 )
                 cols = slice(lo * P, hi * P)
                 nc.vector.quantize_mx(out=codes[:, cols].bitcast(FP8X4), scales=scales[:, cols], in_=part)
@@ -175,8 +176,8 @@ def tile_list_gassing_page_features_kernel(
                 tag = ("x_turned11", "x_woven")[u % 2]
                 woven3[u] = ring.tile([P, W3_WIDTH * PACK], BF16, name="woven3", tag=tag, align_bytes=64)
             nc.scalar.copy(
-                woven3[u][:].rearrange("p (c i t) -> p c t i", i=4, t=PACK),
-                raw3[u][:].rearrange("p t (c i) -> p c t i", i=4),
+                woven3[u][:].rearrange("p (n t) -> p n t", t=PACK),
+                raw3[u][:].rearrange("p t n -> p n t"),
             )
 
         def quantise_w3(u):
@@ -188,20 +189,23 @@ def tile_list_gassing_page_features_kernel(
         def first_products(s):
             a_ps = psum.tile([P, S], F32, name="a_ps", tag="sum_a")
             b_ps = psum.tile([P, S], F32, name="b_ps", tag="sum_b")
-            w2_tile, w2_col = (w2_first, s) if s < W2_FIRST else (w2_rest, s - W2_FIRST)
+            part = [lo <= s < hi for lo, hi in W2_PARTS].index(True)
+            w2_col = 2 * P * (s - W2_PARTS[part][0])
             codes, scales = w1q[s]
             for a in range(PASSES_1):
-                flags = dict(start=(a == 0), stop=(a == PASSES_1 - 1))
-                moving = dict(rhs=v_words[:, a, :].bitcast(FP8X4), rhs_scale=v_sc[:, a, :])
                 nc.tensor.matmul_mx(
                     out=b_ps[:],
-                    lhsT=w2_tile[:, a, 2 * P * w2_col : 2 * P * (w2_col + 1)].bitcast(FP4X4),
+                    lhsT=w2_parts[part][:, a, w2_col : w2_col + 2 * P].bitcast(FP4X4),
                     lhsT_scale=w2_sc[:, a * H + s * P : a * H + (s + 1) * P],
-                    **moving, **flags,
+                    rhs=v_words[:, a, :].bitcast(FP8X4), rhs_scale=v_sc[:, a, :],
+                    start=(a == 0), stop=(a == PASSES_1 - 1),
                 )
+            for a in range(PASSES_1):
                 cols = slice(a * P, (a + 1) * P)
                 nc.tensor.matmul_mx(
-                    out=a_ps[:], lhsT=codes[:, cols].bitcast(FP8X4), lhsT_scale=scales[:, cols], **moving, **flags
+                    out=a_ps[:], lhsT=codes[:, cols].bitcast(FP8X4), lhsT_scale=scales[:, cols],
+                    rhs=v_words[:, a, :].bitcast(FP8X4), rhs_scale=v_sc[:, a, :],
+                    start=(a == 0), stop=(a == PASSES_1 - 1),
                 )
             b_sb = staged(s)[:, 0, :] if s > 0 else z[s]
             nc.scalar.copy(b_sb, b_ps[:])
@@ -217,7 +221,7 @@ def tile_list_gassing_page_features_kernel(
             return stage[n]
 
         def put_state(s):
-            th = staged(anchor(s))[:, 1, :]
+            th = staged(anchor(s) if s > 0 else 0)[:, 1, :]
             nc.scalar.activation(th, z[s], ACT.Tanh)
             nc.vector.tensor_tensor(p0[s][:].indirect(idx2[:]), th, gw[s], ALU.mult)
 

@@ -27,11 +27,12 @@ SLICES_PER_PASS = K_PASS // P
 J_BLOCKS = S // P
 W3_WIDTH = 2 * P
 W3_UNITS = PASSES_2 * H // W3_WIDTH
-W2_PARTS = ((0, 2), (2, 4), (4, 8))
+W2_PARTS = ((0, 1), (1, 3), (3, 8))
 HALF = S // 2
-EARLY = 3
-LATE_SPLIT = 6
-RAMP = 4
+EARLY = 4
+DIRECT = False
+LATE_SPLIT = 7
+RAMP = 3
 
 
 def tile_list_gassing_page_features_kernel(
@@ -115,9 +116,9 @@ def tile_list_gassing_page_features_kernel(
         w2_parts = [load_w2(*W2_PARTS[0])]
         raw1[0] = load_w1(0)
         raw1[1] = load_w1(1)
+        w2_parts.append(load_w2(*W2_PARTS[1]))
         idx2 = load_list("idx2", offs2)
         p0[0] = load_rows("p0_0", page0[0:P, :])
-        w2_parts.append(load_w2(*W2_PARTS[1]))
         raw1[2] = load_w1(2)
         idx3 = load_list("idx3", offs3)
         for s in range(1, SLICES - 2):
@@ -150,7 +151,7 @@ def tile_list_gassing_page_features_kernel(
             nc.scalar.activation(gw[s], wgs_sb[:], ACT.Copy, scale=column(1, s))
         picked_early = [work[s + 1][:, 0:HALF] for s in range(SLICES)]
         x = [work[s + 2][:, HALF : HALF + S] for s in range(SLICES)]
-        x_turned = {}
+        x_turned, turned_ps = {}, {}
         x_codes = [keep.tile([P, S], U32, name="x_codes%d" % b, align_bytes=64) for b in range(PASSES_2)]
         x_scales = [keep.tile([P, S], U8, name="x_scales%d" % b, align_bytes=64) for b in range(PASSES_2)]
 
@@ -158,12 +159,12 @@ def tile_list_gassing_page_features_kernel(
             codes = ring.tile([P, PASSES_1 * P], U32, name="w1_codes", tag="w1_codes", bufs=3, align_bytes=64)
             scales = ring.tile([P, PASSES_1 * P], U8, name="w1_scales", tag="w1_scales", bufs=3, align_bytes=64)
             woven = ring.tile([P, PASSES_1 * K_PASS], BF16, name="woven", tag="woven", bufs=3, align_bytes=64)
-            for lo, hi in ((0, 1), (1, 2), (2, 3)) if s < 2 else ((0, 2), (2, 3)):
+            for lo, hi in ((0, 1), (1, 2), (2, 3)) if s in (0, 1) else ((0, 2), (2, 3)):
                 part = woven[:, lo * K_PASS : hi * K_PASS]
-                weave = nc.vector.tensor_copy if s < 2 else nc.scalar.copy
+                weave = nc.vector.tensor_copy if s == 1 else nc.scalar.copy
                 weave(
-                    part.rearrange("p (a n t) -> p a n t", a=hi - lo, t=PACK),
-                    raw1[s][:, lo:hi, :, :].rearrange("p a t n -> p a n t"),
+                    part.rearrange("p (a c i t) -> p a c t i", a=hi - lo, i=4, t=PACK),
+                    raw1[s][:, lo:hi, :, :].rearrange("p a t (c i) -> p a c t i", i=4),
                 )
                 cols = slice(lo * P, hi * P)
                 nc.vector.quantize_mx(out=codes[:, cols].bitcast(FP8X4), scales=scales[:, cols], in_=part)
@@ -176,8 +177,8 @@ def tile_list_gassing_page_features_kernel(
                 tag = ("x_turned11", "x_woven")[u % 2]
                 woven3[u] = ring.tile([P, W3_WIDTH * PACK], BF16, name="woven3", tag=tag, align_bytes=64)
             nc.scalar.copy(
-                woven3[u][:].rearrange("p (n t) -> p n t", t=PACK),
-                raw3[u][:].rearrange("p t n -> p n t"),
+                woven3[u][:].rearrange("p (c i t) -> p c t i", i=4, t=PACK),
+                raw3[u][:].rearrange("p t (c i) -> p c t i", i=4),
             )
 
         def quantise_w3(u):
@@ -207,7 +208,7 @@ def tile_list_gassing_page_features_kernel(
                     rhs=v_words[:, a, :].bitcast(FP8X4), rhs_scale=v_sc[:, a, :],
                     start=(a == 0), stop=(a == PASSES_1 - 1),
                 )
-            b_sb = staged(s)[:, 0, :] if s > 0 else z[s]
+            b_sb = staged(s)[:, 0, :]
             nc.scalar.copy(b_sb, b_ps[:])
             nc.vector.scalar_tensor_tensor(z[s], a_ps[:], column(0, s), b_sb, ALU.mult, ALU.add)
 
@@ -231,21 +232,35 @@ def tile_list_gassing_page_features_kernel(
         def recall(s, half, picked):
             nc.vector.tensor_copy(picked, p0[s][:].indirect(list_half(idx3, half)))
 
-        def turn(s, half, picked):
+        def add_shift(s, half, picked):
+            nc.scalar.activation(x[s][:, half * HALF : (half + 1) * HALF], picked, ACT.Identity, bias=column(2, s))
+
+        def turn(s, half, picked, direct):
             b, q = divmod(s, SLICES_PER_PASS)
-            x_half = x[s][:, half * HALF : (half + 1) * HALF]
-            nc.scalar.activation(x_half, picked, ACT.Identity, bias=column(2, s))
-            turned_ps = psum.tile([P, 2, P], F32, name="turned_ps", tag="turn")
+            if q % 2 == 0:
+                turned_ps[half] = psum.tile([P, 2, 2, P], F32, name="turned_ps", tag="turn")
+            if not direct:
+                add_shift(s, half, picked)
             for c in range(2):
-                nc.tensor.transpose(turned_ps[:, c, :], x_half[:, c * P : (c + 1) * P], ident[:])
+                block = turned_ps[half][:, c, q % 2, :]
+                if direct:
+                    spread = column(2, s).to_broadcast([P, P])
+                    nc.tensor.matmul(block, spread, ident[:], start=True, stop=False, is_transpose=True)
+                    nc.tensor.matmul(
+                        block, picked[:, c * P : (c + 1) * P], ident[:], start=False, stop=True, is_transpose=True
+                    )
+                else:
+                    first = half * HALF + c * P
+                    nc.tensor.transpose(block, x[s][:, first : first + P], ident[:])
             if q == 0:
                 x_turned[half, b] = ring.tile(
                     [P, 2, 2, SLICES_PER_PASS, 32, 2], BF16, name="x_turned%d%d" % (half, b), align_bytes=64
                 )
-            nc.scalar.copy(
-                x_turned[half, b][:, :, :, q, :, :],
-                turned_ps[:].rearrange("j c (m u e) -> j c u m e", u=2, e=2),
-            )
+            if q % 2 == 1:
+                nc.scalar.copy(
+                    x_turned[half, b][:, :, :, q - 1 : q + 1, :, :].rearrange("j c u q m e -> j c u (q m) e"),
+                    turned_ps[half][:].rearrange("j c q (m u e) -> j c u (q m) e", u=2, e=2),
+                )
             if q == SLICES_PER_PASS - 1:
                 quantise_x(half, b)
 
@@ -306,7 +321,7 @@ def tile_list_gassing_page_features_kernel(
                 first_products(ahead)
                 done = ahead
             if s > 1:
-                turn(s - 2, 0, picked_early[s - 2])
+                turn(s - 2, 0, picked_early[s - 2], False)
         wgo_sb = load_rows("wgo_sb", wgo)
         idx4 = load_list("idx4", offs4)
         for s in range(EARLY):
@@ -317,17 +332,24 @@ def tile_list_gassing_page_features_kernel(
             p1[s] = load_p1(s)
         recall(SLICES - 1, 0, picked_early[SLICES - 1])
         for s in (SLICES - 2, SLICES - 1):
-            turn(s, 0, picked_early[s])
+            turn(s, 0, picked_early[s], DIRECT)
         for s in range(EARLY - 1):
             second_stage(s, 0, HALF, x[s][:, 0:HALF])
+        picked_late = []
         late0 = ring.tile([P, LATE_SPLIT, HALF], F32, name="picked_late0", tag="slot3")
         late1 = ring.tile([P, SLICES - LATE_SPLIT, HALF], F32, name="picked_late1", tag="late2", align_bytes=64)
         for s in range(SLICES):
             picked = late0[:, s, :] if s < LATE_SPLIT else late1[:, s - LATE_SPLIT, :]
             recall(s, 1, picked)
-            turn(s, 1, picked)
+            turn(s, 1, picked, DIRECT)
+            picked_late.append(picked)
         for s in range(EARLY - 1):
             put_features(s, 0, HALF, x[s][:, 0:HALF])
+        if DIRECT:
+            for s in range(SLICES):
+                add_shift(s, 1, picked_late[s])
+            for s in (SLICES - 2, SLICES - 1):
+                add_shift(s, 0, picked_early[s])
         filler = ring.tile([P, HALF], F32, name="y_early", tag="x_woven", align_bytes=64)
         second_stage(EARLY - 1, 0, HALF, filler[:])
         put_features(EARLY - 1, 0, HALF, filler[:])

@@ -24,15 +24,23 @@ PASSES_1 = K // K_PASS
 PASSES_2 = H // K_PASS
 SLICES = H // P
 SLICES_PER_PASS = K_PASS // P
-J_BLOCKS = S // P
-W3_WIDTH = 2 * P
-W3_UNITS = PASSES_2 * H // W3_WIDTH
-W2_PARTS = ((0, 1), (1, 3), (3, 8))
+GROUP = 16
+LINE = 4
 HALF = S // 2
-EARLY = 4
-DIRECT = False
-LATE_SPLIT = 7
+
+PIECE_WIDTH = 2 * P
+PIECES = PASSES_2 * H // PIECE_WIDTH
+PIECES_BEFORE = PIECES // 2
+
+W2_PARTS = ((0, 1), (1, 3), (3, SLICES))
 RAMP = 3
+TURN_LAG = 3
+EARLY = 4
+LATE_SPLIT = 6
+OWN_PAGES = 4
+PAGE_BUFFERS = (0, 2, 4, 5)
+
+SENS, GAIN, SHIFT, BACK = 0, 1, 2, 3
 
 
 def tile_list_gassing_page_features_kernel(
@@ -42,11 +50,17 @@ def tile_list_gassing_page_features_kernel(
     nc = tc.nc
     with ExitStack() as ctx:
         keep = ctx.enter_context(tc.tile_pool(name="keep", bufs=1))
-        ring = ctx.enter_context(tc.tile_pool(name="ring", bufs=1))
+        reuse = ctx.enter_context(tc.tile_pool(name="reuse", bufs=1))
         psum = ctx.enter_context(tc.psum_pool(name="psum", bufs=2))
 
+        def staging(n):
+            return "staging%d" % n
+
+        def rows_of(s):
+            return slice(s * P, (s + 1) * P)
+
         def load_list(name, source):
-            tile = keep.tile([P, S // 16], U16, name=name)
+            tile = keep.tile([P, S // GROUP], U16, name=name)
             nc.sync.dma_start(tile[:], source)
             return tile
 
@@ -60,25 +74,22 @@ def tile_list_gassing_page_features_kernel(
                 )
             return tile
 
-        def load_tab(lo, hi):
-            tile = keep.tile([P, (hi - lo) * T], U32, name="tab%d" % lo)
-            nc.sync.dma_start(
-                tile[:].bitcast(I32).rearrange("p (a t) -> p a t", a=hi - lo),
-                tab_words[lo:hi].rearrange("a p t i -> p a (t i)").bitcast(I32),
-            )
-            return [tile[:, a * T : (a + 1) * T] for a in range(hi - lo)]
+        def load_table(a):
+            tile = keep.tile([P, T], U32, name="table%d" % a)
+            nc.sync.dma_start(tile[:].bitcast(I32), tab_words[a].rearrange("p t i -> p (t i)").bitcast(I32))
+            return tile
 
         def load_w1(s):
-            tile = ring.tile([P, PASSES_1, PACK, P], F32, name="raw1", tag="slot%d" % s)
+            tile = reuse.tile([P, PASSES_1, PACK, P], F32, name="w1_raw", tag=staging(s))
             for a in range(PASSES_1):
-                rows = w1[a * K_PASS : (a + 1) * K_PASS, s * P : (s + 1) * P]
+                rows = w1[a * K_PASS : (a + 1) * K_PASS, rows_of(s)]
                 nc.sync.dma_start(tile[:, a, :, :], rows.rearrange("(p t) n -> p t n", t=PACK))
             return tile
 
-        def load_w3(u):
-            c, b = divmod(u, PASSES_2)
-            tile = ring.tile([P, PACK, W3_WIDTH], F32, name="raw3", tag="slot%d" % u)
-            rows = w3[b * K_PASS : (b + 1) * K_PASS, c * W3_WIDTH : (c + 1) * W3_WIDTH]
+        def load_w3(piece):
+            c, b = divmod(piece, PASSES_2)
+            tile = reuse.tile([P, PACK, PIECE_WIDTH], F32, name="w3_raw", tag=staging(piece))
+            rows = w3[b * K_PASS : (b + 1) * K_PASS, c * PIECE_WIDTH : (c + 1) * PIECE_WIDTH]
             nc.sync.dma_start(tile[:], rows.rearrange("(p t) n -> p t n", t=PACK))
             return tile
 
@@ -95,44 +106,48 @@ def tile_list_gassing_page_features_kernel(
             nc.sync.dma_start(tile[:], source)
             return tile
 
-        def load_p1(s):
-            tile = ring.tile([P, T2], F32, name="p1", tag="p1_%d" % s if s < 4 else "slot%d" % (0, 2, 4, 5)[s - 4])
-            nc.sync.dma_start(tile[:], page1[s * P : (s + 1) * P, :])
+        def load_page0(s):
+            return load_rows("page0_%d" % s, page0[rows_of(s), :])
+
+        def load_page1(s):
+            tag = "page1_%d" % s if s < OWN_PAGES else staging(PAGE_BUFFERS[s - OWN_PAGES])
+            tile = reuse.tile([P, T2], F32, name="page1_tile", tag=tag)
+            nc.sync.dma_start(tile[:], page1[rows_of(s), :])
             return tile
 
-        raw1, raw3, p0, p1 = {}, {}, {}, {}
+        w1_raw, w3_raw, state_page, out_page = {}, {}, {}, {}
         idx = load_list("idx", offs)
         wgs_sb = load_rows("wgs_sb", wgs)
-        tab = load_tab(0, 1)
+        table = [load_table(0)]
         vec_rows = keep.tile([P, P], F32, name="vec_rows")
         nc.gpsimd.memset(vec_rows[:], 0.0)
         for v, vec in enumerate((sens, gain, shift, back)):
             nc.scalar.dma_start(vec_rows[SLICES * v : SLICES * (v + 1), :], vec.rearrange("(s p) -> s p", p=P))
         ident = keep.tile([P, P], F32, name="ident")
         make_identity(nc, ident[:])
-        tab_sc = load_scale_rows("tab_sc", tab_scales, T, nc.scalar)
-        tab = tab + load_tab(1, 2) + load_tab(2, 3)
+        table_scales = load_scale_rows("table_scales", tab_scales, T, nc.scalar)
+        table = table + [load_table(1), load_table(2)]
         w2_sc = load_scale_rows("w2_sc", w2_scales, H, nc.sync)
         w2_parts = [load_w2(*W2_PARTS[0])]
-        raw1[0] = load_w1(0)
-        raw1[1] = load_w1(1)
+        w1_raw[0] = load_w1(0)
+        w1_raw[1] = load_w1(1)
         w2_parts.append(load_w2(*W2_PARTS[1]))
         idx2 = load_list("idx2", offs2)
-        p0[0] = load_rows("p0_0", page0[0:P, :])
-        raw1[2] = load_w1(2)
+        state_page[0] = load_page0(0)
+        w1_raw[2] = load_w1(2)
         idx3 = load_list("idx3", offs3)
         for s in range(1, SLICES - 2):
-            p0[s] = load_rows("p0_%d" % s, page0[s * P : (s + 1) * P, :])
+            state_page[s] = load_page0(s)
             if s + 2 == W2_PARTS[2][0]:
                 w2_parts.append(load_w2(*W2_PARTS[2]))
-            raw1[s + 2] = load_w1(s + 2)
+            w1_raw[s + 2] = load_w1(s + 2)
 
         v_words = keep.tile([P, PASSES_1, S], U32, name="v_words", align_bytes=64)
-        v_sc = keep.tile([P, PASSES_1, S], U8, name="v_sc", align_bytes=64)
+        v_scales = keep.tile([P, PASSES_1, S], U8, name="v_scales", align_bytes=64)
         for a in range(PASSES_1):
-            nc.vector.tensor_copy(v_sc[:, a, :], tab_sc[:, a * T : (a + 1) * T].indirect(idx[:]))
+            nc.vector.tensor_copy(v_scales[:, a, :], table_scales[:, a * T : (a + 1) * T].indirect(idx[:]))
         for a in range(PASSES_1):
-            nc.vector.tensor_copy(v_words[:, a, :], tab[a].indirect(idx[:]))
+            nc.vector.tensor_copy(v_words[:, a, :], table[a][:].indirect(idx[:]))
 
         vec_ps = psum.tile([P, P], F32, name="vec_ps", tag="turn")
         nc.tensor.transpose(vec_ps[:], vec_rows[:], ident[:])
@@ -142,118 +157,104 @@ def tile_list_gassing_page_features_kernel(
         def column(v, s):
             return vec_cols[:, SLICES * v + s : SLICES * v + s + 1]
 
-        w1q, w3q, woven3 = {}, {}, {}
-        stage = {}
-        work = [keep.tile([P, S + HALF], F32, name="work%d" % s) for s in range(SLICES + 2)]
+        def ahead_of(s):
+            return s + 2 if s >= RAMP else s + 1
+
+        work = [keep.tile([P, S + HALF], F32, name="work%d" % n) for n in range(SLICES + TURN_LAG)]
         z = [work[s][:, 0:S] for s in range(SLICES)]
-        gw = [work[s + 2 if s > RAMP else s + 1][:, 0:S] for s in range(SLICES)]
+        gain_wgs = [work[s + 2 if s > RAMP else s + 1][:, 0:S] for s in range(SLICES)]
         for s in range(SLICES):
-            nc.scalar.activation(gw[s], wgs_sb[:], ACT.Copy, scale=column(1, s))
-        picked_early = [work[s + 1][:, 0:HALF] for s in range(SLICES)]
-        x = [work[s + 2][:, HALF : HALF + S] for s in range(SLICES)]
-        x_turned, turned_ps = {}, {}
+            nc.scalar.activation(gain_wgs[s], wgs_sb[:], ACT.Copy, scale=column(GAIN, s))
+        picked_first = [work[s + 1][:, 0:HALF] for s in range(SLICES)]
+        x = [work[s + TURN_LAG][:, HALF : HALF + S] for s in range(SLICES)]
         x_codes = [keep.tile([P, S], U32, name="x_codes%d" % b, align_bytes=64) for b in range(PASSES_2)]
         x_scales = [keep.tile([P, S], U8, name="x_scales%d" % b, align_bytes=64) for b in range(PASSES_2)]
+        w1_mx, w3_mx, pair_tiles, x_turned, turned_ps = {}, {}, {}, {}, {}
+
+        def pair_tile(n):
+            if n not in pair_tiles:
+                buffer = n if n < SLICES else PASSES_2 * (n - SLICES) + 1
+                pair_tiles[n] = reuse.tile([P, 2, S], F32, name="pair_tile", tag=staging(buffer))
+            return pair_tiles[n]
 
         def quantise_w1(s):
-            codes = ring.tile([P, PASSES_1 * P], U32, name="w1_codes", tag="w1_codes", bufs=3, align_bytes=64)
-            scales = ring.tile([P, PASSES_1 * P], U8, name="w1_scales", tag="w1_scales", bufs=3, align_bytes=64)
-            woven = ring.tile([P, PASSES_1 * K_PASS], BF16, name="woven", tag="woven", bufs=3, align_bytes=64)
-            for lo, hi in ((0, 1), (1, 2), (2, 3)) if s in (0, 1) else ((0, 2), (2, 3)):
+            codes = reuse.tile([P, PASSES_1 * P], U32, name="w1_codes", tag="w1_codes", bufs=3, align_bytes=64)
+            scales = reuse.tile([P, PASSES_1 * P], U8, name="w1_scales", tag="w1_scales", bufs=3, align_bytes=64)
+            woven = reuse.tile([P, PASSES_1 * K_PASS], BF16, name="w1_woven", tag="woven", bufs=3, align_bytes=64)
+            weave = nc.vector.tensor_copy if s == 1 else nc.scalar.copy
+            for lo, hi in ((0, 1), (1, 2), (2, 3)) if s < 2 else ((0, 2), (2, 3)):
                 part = woven[:, lo * K_PASS : hi * K_PASS]
-                weave = nc.vector.tensor_copy if s == 1 else nc.scalar.copy
                 weave(
-                    part.rearrange("p (a c i t) -> p a c t i", a=hi - lo, i=4, t=PACK),
-                    raw1[s][:, lo:hi, :, :].rearrange("p a t (c i) -> p a c t i", i=4),
+                    part.rearrange("p (a c i t) -> p a c t i", a=hi - lo, i=LINE, t=PACK),
+                    w1_raw[s][:, lo:hi, :, :].rearrange("p a t (c i) -> p a c t i", i=LINE),
                 )
                 cols = slice(lo * P, hi * P)
                 nc.vector.quantize_mx(out=codes[:, cols].bitcast(FP8X4), scales=scales[:, cols], in_=part)
-            w1q[s] = codes, scales
+            w1_mx[s] = codes, scales
 
-        def weave_w3(u):
-            if u < 4:
-                woven3[u] = ring.tile([P, W3_WIDTH * PACK], BF16, name="woven3", tag="woven", bufs=3, align_bytes=64)
+        def quantise_w3(piece):
+            shape = [P, PIECE_WIDTH * PACK]
+            if piece < PIECES_BEFORE:
+                woven = reuse.tile(shape, BF16, name="w3_woven", tag="woven", bufs=3, align_bytes=64)
             else:
-                tag = ("x_turned11", "x_woven")[u % 2]
-                woven3[u] = ring.tile([P, W3_WIDTH * PACK], BF16, name="woven3", tag=tag, align_bytes=64)
+                tag = ("x_turned11", "x_woven11")[piece % 2]
+                woven = reuse.tile(shape, BF16, name="w3_woven", tag=tag, align_bytes=64)
             nc.scalar.copy(
-                woven3[u][:].rearrange("p (c i t) -> p c t i", i=4, t=PACK),
-                raw3[u][:].rearrange("p t (c i) -> p c t i", i=4),
+                woven[:].rearrange("p (c i t) -> p c t i", i=LINE, t=PACK),
+                w3_raw[piece][:].rearrange("p t (c i) -> p c t i", i=LINE),
             )
-
-        def quantise_w3(u):
-            codes = keep.tile([P, W3_WIDTH], U32, name="w3_codes%d" % u, align_bytes=64)
-            scales = keep.tile([P, W3_WIDTH], U8, name="w3_scales%d" % u, align_bytes=64)
-            nc.vector.quantize_mx(out=codes[:].bitcast(FP8X4), scales=scales[:], in_=woven3[u][:])
-            w3q[u] = codes, scales
+            codes = keep.tile([P, PIECE_WIDTH], U32, name="w3_codes%d" % piece, align_bytes=64)
+            scales = keep.tile([P, PIECE_WIDTH], U8, name="w3_scales%d" % piece, align_bytes=64)
+            nc.vector.quantize_mx(out=codes[:].bitcast(FP8X4), scales=scales[:], in_=woven[:])
+            w3_mx[piece] = codes, scales
 
         def first_products(s):
             a_ps = psum.tile([P, S], F32, name="a_ps", tag="sum_a")
             b_ps = psum.tile([P, S], F32, name="b_ps", tag="sum_b")
             part = [lo <= s < hi for lo, hi in W2_PARTS].index(True)
-            w2_col = 2 * P * (s - W2_PARTS[part][0])
-            codes, scales = w1q[s]
+            w2_byte = 2 * P * (s - W2_PARTS[part][0])
+            codes, scales = w1_mx[s]
             for a in range(PASSES_1):
                 nc.tensor.matmul_mx(
                     out=b_ps[:],
-                    lhsT=w2_parts[part][:, a, w2_col : w2_col + 2 * P].bitcast(FP4X4),
+                    lhsT=w2_parts[part][:, a, w2_byte : w2_byte + 2 * P].bitcast(FP4X4),
                     lhsT_scale=w2_sc[:, a * H + s * P : a * H + (s + 1) * P],
-                    rhs=v_words[:, a, :].bitcast(FP8X4), rhs_scale=v_sc[:, a, :],
+                    rhs=v_words[:, a, :].bitcast(FP8X4), rhs_scale=v_scales[:, a, :],
                     start=(a == 0), stop=(a == PASSES_1 - 1),
                 )
             for a in range(PASSES_1):
                 cols = slice(a * P, (a + 1) * P)
                 nc.tensor.matmul_mx(
                     out=a_ps[:], lhsT=codes[:, cols].bitcast(FP8X4), lhsT_scale=scales[:, cols],
-                    rhs=v_words[:, a, :].bitcast(FP8X4), rhs_scale=v_sc[:, a, :],
+                    rhs=v_words[:, a, :].bitcast(FP8X4), rhs_scale=v_scales[:, a, :],
                     start=(a == 0), stop=(a == PASSES_1 - 1),
                 )
-            b_sb = staged(s)[:, 0, :]
+            b_sb = pair_tile(s)[:, 0, :]
             nc.scalar.copy(b_sb, b_ps[:])
-            nc.vector.scalar_tensor_tensor(z[s], a_ps[:], column(0, s), b_sb, ALU.mult, ALU.add)
-
-        def anchor(s):
-            return s + 2 if s >= RAMP else s + 1
-
-        def staged(n):
-            if n not in stage:
-                slot = n if n < SLICES else 2 * (n - SLICES) + 1
-                stage[n] = ring.tile([P, 2, S], F32, name="stage", tag="slot%d" % slot)
-            return stage[n]
+            nc.vector.scalar_tensor_tensor(z[s], a_ps[:], column(SENS, s), b_sb, ALU.mult, ALU.add)
 
         def put_state(s):
-            th = staged(anchor(s) if s > 0 else 0)[:, 1, :]
-            nc.scalar.activation(th, z[s], ACT.Tanh)
-            nc.vector.tensor_tensor(p0[s][:].indirect(idx2[:]), th, gw[s], ALU.mult)
-
-        def list_half(offsets, half):
-            return offsets[:, half * HALF // 16 : (half + 1) * HALF // 16]
+            tanh_z = pair_tile(ahead_of(s) if s > 0 else 0)[:, 1, :]
+            nc.scalar.activation(tanh_z, z[s], ACT.Tanh)
+            nc.vector.tensor_tensor(state_page[s][:].indirect(idx2[:]), tanh_z, gain_wgs[s], ALU.mult)
 
         def recall(s, half, picked):
-            nc.vector.tensor_copy(picked, p0[s][:].indirect(list_half(idx3, half)))
+            offsets = idx3[:, half * HALF // GROUP : (half + 1) * HALF // GROUP]
+            nc.vector.tensor_copy(picked, state_page[s][:].indirect(offsets))
 
         def add_shift(s, half, picked):
-            nc.scalar.activation(x[s][:, half * HALF : (half + 1) * HALF], picked, ACT.Identity, bias=column(2, s))
+            x_half = x[s][:, half * HALF : (half + 1) * HALF]
+            nc.scalar.activation(x_half, picked, ACT.Identity, bias=column(SHIFT, s))
 
-        def turn(s, half, picked, direct):
+        def turn(s, half):
             b, q = divmod(s, SLICES_PER_PASS)
             if q % 2 == 0:
                 turned_ps[half] = psum.tile([P, 2, 2, P], F32, name="turned_ps", tag="turn")
-            if not direct:
-                add_shift(s, half, picked)
             for c in range(2):
-                block = turned_ps[half][:, c, q % 2, :]
-                if direct:
-                    spread = column(2, s).to_broadcast([P, P])
-                    nc.tensor.matmul(block, spread, ident[:], start=True, stop=False, is_transpose=True)
-                    nc.tensor.matmul(
-                        block, picked[:, c * P : (c + 1) * P], ident[:], start=False, stop=True, is_transpose=True
-                    )
-                else:
-                    first = half * HALF + c * P
-                    nc.tensor.transpose(block, x[s][:, first : first + P], ident[:])
+                first = half * HALF + c * P
+                nc.tensor.transpose(turned_ps[half][:, c, q % 2, :], x[s][:, first : first + P], ident[:])
             if q == 0:
-                x_turned[half, b] = ring.tile(
+                x_turned[half, b] = reuse.tile(
                     [P, 2, 2, SLICES_PER_PASS, 32, 2], BF16, name="x_turned%d%d" % (half, b), align_bytes=64
                 )
             if q % 2 == 1:
@@ -266,8 +267,8 @@ def tile_list_gassing_page_features_kernel(
 
         def quantise_x(half, b):
             words = x_turned[half, b][:].rearrange("j c u q m e -> j (c u q m e)").bitcast(F32)
-            tag = "x_woven_first" if b == 0 else ("late2", "x_woven")[half]
-            woven = ring.tile([P, HALF * PACK], BF16, name="x_woven", tag=tag, align_bytes=64)
+            tag = "x_woven_pass0" if b == 0 else "x_woven%d1" % half
+            woven = reuse.tile([P, HALF * PACK], BF16, name="x_woven", tag=tag, align_bytes=64)
             back_ps = psum.tile([P, 2, 2, P], F32, name="back_ps", tag="turn_back")
             for c in range(2):
                 for u in range(2):
@@ -280,92 +281,84 @@ def tile_list_gassing_page_features_kernel(
             cols = slice(half * HALF, (half + 1) * HALF)
             nc.vector.quantize_mx(out=x_codes[b][:, cols].bitcast(FP8X4), scales=x_scales[b][:, cols], in_=woven[:])
 
-        def second_stage(s, lo, hi, result):
+        def last_product(s, lo, hi, y):
             e_ps = psum.tile([P, hi - lo], F32, name="e_ps", tag=("sum_a", "sum_b")[s % 2])
+            cols = slice((s % 2) * P, (s % 2 + 1) * P)
             for b in reversed(range(PASSES_2)):
-                codes, scales = w3q[PASSES_2 * (s // 2) + b]
-                cols = slice((s % 2) * P, (s % 2 + 1) * P)
+                codes, scales = w3_mx[PASSES_2 * (s // 2) + b]
                 nc.tensor.matmul_mx(
                     out=e_ps[:], lhsT=codes[:, cols].bitcast(FP8X4), lhsT_scale=scales[:, cols],
                     rhs=x_codes[b][:, lo:hi].bitcast(FP8X4), rhs_scale=x_scales[b][:, lo:hi],
                     start=(b == PASSES_2 - 1), stop=(b == 0),
                 )
-            nc.vector.scalar_tensor_tensor(result, x[s][:, lo:hi], column(3, s), e_ps[:], ALU.mult, ALU.max)
+            nc.vector.scalar_tensor_tensor(y, x[s][:, lo:hi], column(BACK, s), e_ps[:], ALU.mult, ALU.max)
 
-        def put_features(s, lo, hi, values):
-            offsets = idx4[:, lo // 16 : hi // 16]
-            nc.vector.tensor_tensor(p1[s][:].indirect(offsets), values, wgo_sb[:, lo:hi], ALU.mult)
+        def put_features(s, lo, hi, y):
+            offsets = idx4[:, lo // GROUP : hi // GROUP]
+            nc.vector.tensor_tensor(out_page[s][:].indirect(offsets), y, wgo_sb[:, lo:hi], ALU.mult)
             if hi == S:
-                nc.sync.dma_start(out[s * P : (s + 1) * P, :], p1[s][:])
-
-        def prepare_w3(u):
-            raw3[u] = load_w3(u)
-            weave_w3(u)
-            quantise_w3(u)
+                nc.sync.dma_start(out[rows_of(s), :], out_page[s][:])
 
         quantise_w1(0)
         first_products(0)
-        done = 0
+        multiplied = 0
         for s in range(SLICES):
-            for ahead in range(anchor(s - 1) + 1, anchor(s) + 1):
-                if ahead < SLICES:
-                    quantise_w1(ahead)
+            for n in range(ahead_of(s - 1) + 1, ahead_of(s) + 1):
+                if n < SLICES:
+                    quantise_w1(n)
                 else:
-                    prepare_w3(2 * (ahead - SLICES))
-                    prepare_w3(2 * (ahead - SLICES) + 1)
-                    p0[s] = load_rows("p0_%d" % s, page0[s * P : (s + 1) * P, :])
+                    for piece in range(PASSES_2 * (n - SLICES), PASSES_2 * (n - SLICES + 1)):
+                        w3_raw[piece] = load_w3(piece)
+                        quantise_w3(piece)
+                    state_page[s] = load_page0(s)
             put_state(s)
             if s > 0:
-                recall(s - 1, 0, picked_early[s - 1])
-            for ahead in range(done + 1, min(anchor(s), SLICES - 1) + 1):
-                first_products(ahead)
-                done = ahead
-            if s > 1:
-                turn(s - 2, 0, picked_early[s - 2], False)
+                recall(s - 1, 0, picked_first[s - 1])
+            for n in range(multiplied + 1, min(ahead_of(s), SLICES - 1) + 1):
+                first_products(n)
+                multiplied = n
+            if s >= TURN_LAG:
+                add_shift(s - TURN_LAG, 0, picked_first[s - TURN_LAG])
+                turn(s - TURN_LAG, 0)
+
         wgo_sb = load_rows("wgo_sb", wgo)
         idx4 = load_list("idx4", offs4)
         for s in range(EARLY):
-            p1[s] = load_p1(s)
-        for u in range(4, W3_UNITS):
-            raw3[u] = load_w3(u)
+            out_page[s] = load_page1(s)
+        for piece in range(PIECES_BEFORE, PIECES):
+            w3_raw[piece] = load_w3(piece)
         for s in range(EARLY, SLICES - 2):
-            p1[s] = load_p1(s)
-        recall(SLICES - 1, 0, picked_early[SLICES - 1])
-        for s in (SLICES - 2, SLICES - 1):
-            turn(s, 0, picked_early[s], DIRECT)
+            out_page[s] = load_page1(s)
+
+        for s in range(SLICES - TURN_LAG, SLICES):
+            if s == SLICES - 2:
+                recall(SLICES - 1, 0, picked_first[SLICES - 1])
+            add_shift(s, 0, picked_first[s])
+            turn(s, 0)
         for s in range(EARLY - 1):
-            second_stage(s, 0, HALF, x[s][:, 0:HALF])
-        picked_late = []
-        late0 = ring.tile([P, LATE_SPLIT, HALF], F32, name="picked_late0", tag="slot3")
-        late1 = ring.tile([P, SLICES - LATE_SPLIT, HALF], F32, name="picked_late1", tag="late2", align_bytes=64)
+            last_product(s, 0, HALF, x[s][:, 0:HALF])
+
+        picked_a = reuse.tile([P, LATE_SPLIT, HALF], F32, name="picked_a", tag=staging(PIECES_BEFORE - 1))
+        picked_b = reuse.tile([P, SLICES - LATE_SPLIT, HALF], F32, name="picked_b", tag="x_woven01", align_bytes=64)
         for s in range(SLICES):
-            picked = late0[:, s, :] if s < LATE_SPLIT else late1[:, s - LATE_SPLIT, :]
+            picked = picked_a[:, s, :] if s < LATE_SPLIT else picked_b[:, s - LATE_SPLIT, :]
             recall(s, 1, picked)
-            turn(s, 1, picked, DIRECT)
-            picked_late.append(picked)
+            add_shift(s, 1, picked)
+        for s in range(SLICES):
+            turn(s, 1)
         for s in range(EARLY - 1):
             put_features(s, 0, HALF, x[s][:, 0:HALF])
-        if DIRECT:
-            for s in range(SLICES):
-                add_shift(s, 1, picked_late[s])
-            for s in (SLICES - 2, SLICES - 1):
-                add_shift(s, 0, picked_early[s])
-        filler = ring.tile([P, HALF], F32, name="y_early", tag="x_woven", align_bytes=64)
-        second_stage(EARLY - 1, 0, HALF, filler[:])
-        put_features(EARLY - 1, 0, HALF, filler[:])
-        for u in range(4, W3_UNITS):
-            weave_w3(u)
-            quantise_w3(u)
+        y_after = reuse.tile([P, HALF], F32, name="y_after", tag="x_woven11", align_bytes=64)
+        last_product(EARLY - 1, 0, HALF, y_after[:])
+        put_features(EARLY - 1, 0, HALF, y_after[:])
+        for piece in range(PIECES_BEFORE, PIECES):
+            quantise_w3(piece)
         for s in range(SLICES - 2, SLICES):
-            p1[s] = load_p1(s)
+            out_page[s] = load_page1(s)
 
-        def start_second(s):
-            lo = HALF if s < EARLY else 0
-            second_stage(s, lo, S, x[s][:, lo:S])
-
-        start_second(0)
+        first_entry = [HALF if s < EARLY else 0 for s in range(SLICES)]
+        last_product(0, first_entry[0], S, x[0][:, first_entry[0] : S])
         for s in range(SLICES):
             if s + 1 < SLICES:
-                start_second(s + 1)
-            lo = HALF if s < EARLY else 0
-            put_features(s, lo, S, x[s][:, lo:S])
+                last_product(s + 1, first_entry[s + 1], S, x[s + 1][:, first_entry[s + 1] : S])
+            put_features(s, first_entry[s], S, x[s][:, first_entry[s] : S])

from contextlib import ExitStack

import concourse.mybir as mybir
from concourse.masks import make_identity

K, H, T, S, T2 = 1536, 1024, 2048, 512, 1024
FLOPS = 2 * S * (2 * K * H + H * H)

F32 = mybir.dt.float32
BF16 = mybir.dt.bfloat16
I32 = mybir.dt.int32
U32 = mybir.dt.uint32
U16 = mybir.dt.uint16
U8 = mybir.dt.uint8
FP8X4 = mybir.dt.float8_e4m3fn_x4
FP4X4 = mybir.dt.float4_e2m1fn_x4
ALU = mybir.AluOpType
ACT = mybir.ActivationFunctionType

P = 128
PACK = 4
K_PASS = P * PACK
PASSES_1 = K // K_PASS
PASSES_2 = H // K_PASS
SLICES = H // P
SLICES_PER_PASS = K_PASS // P
GROUP = 16
LINE = 4
HALF = S // 2

PIECE_WIDTH = 2 * P
PIECES = PASSES_2 * H // PIECE_WIDTH
PIECES_BEFORE = PIECES // 2

W2_PARTS = ((0, 1), (1, 3), (3, SLICES))
RAMP = 3
TURN_LAG = 3
EARLY = 4
LATE_SPLIT = 6
OWN_PAGES = 4
PAGE_BUFFERS = (0, 2, 4, 5)

SENS, GAIN, SHIFT, BACK = 0, 1, 2, 3


def tile_list_gassing_page_features_kernel(
    tc, tab_words, tab_scales, offs, w1, w2_words, w2_scales, sens, gain, wgs, page0,
    offs2, offs3, shift, w3, back, wgo, page1, offs4, out,
):
    nc = tc.nc
    with ExitStack() as ctx:
        keep = ctx.enter_context(tc.tile_pool(name="keep", bufs=1))
        reuse = ctx.enter_context(tc.tile_pool(name="reuse", bufs=1))
        psum = ctx.enter_context(tc.psum_pool(name="psum", bufs=2))

        def staging(n):
            return "staging%d" % n

        def rows_of(s):
            return slice(s * P, (s + 1) * P)

        def load_list(name, source):
            tile = keep.tile([P, S // GROUP], U16, name=name)
            nc.sync.dma_start(tile[:], source)
            return tile

        def load_scale_rows(name, source, width, queue):
            tile = keep.tile([P, PASSES_1 * width], U8, name=name, align_bytes=64)
            nc.vector.memset(tile[:].bitcast(I32), 0)
            for q in range(4):
                queue.dma_start(
                    tile[32 * q : 32 * q + 4, :].bitcast(I32).rearrange("r (a c) -> r a c", a=PASSES_1),
                    source[:, 4 * q : 4 * q + 4, :].bitcast(I32).rearrange("a r c -> r a c"),
                )
            return tile

        def load_table(a):
            tile = keep.tile([P, T], U32, name="table%d" % a)
            nc.sync.dma_start(tile[:].bitcast(I32), tab_words[a].rearrange("p t i -> p (t i)").bitcast(I32))
            return tile

        def load_w1(s):
            tile = reuse.tile([P, PASSES_1, PACK, P], F32, name="w1_raw", tag=staging(s))
            for a in range(PASSES_1):
                rows = w1[a * K_PASS : (a + 1) * K_PASS, rows_of(s)]
                nc.sync.dma_start(tile[:, a, :, :], rows.rearrange("(p t) n -> p t n", t=PACK))
            return tile

        def load_w3(piece):
            c, b = divmod(piece, PASSES_2)
            tile = reuse.tile([P, PACK, PIECE_WIDTH], F32, name="w3_raw", tag=staging(piece))
            rows = w3[b * K_PASS : (b + 1) * K_PASS, c * PIECE_WIDTH : (c + 1) * PIECE_WIDTH]
            nc.sync.dma_start(tile[:], rows.rearrange("(p t) n -> p t n", t=PACK))
            return tile

        def load_w2(lo, hi):
            tile = keep.tile([P, PASSES_1, 2 * (hi - lo) * P], U8, name="w2_%d" % lo, align_bytes=64)
            nc.sync.dma_start(
                tile[:].bitcast(I32),
                w2_words[:, :, 2 * lo * P : 2 * hi * P].bitcast(I32).rearrange("a p c -> p a c"),
            )
            return tile

        def load_rows(name, source):
            tile = keep.tile([P, source.shape[1]], F32, name=name)
            nc.sync.dma_start(tile[:], source)
            return tile

        def load_page0(s):
            return load_rows("page0_%d" % s, page0[rows_of(s), :])

        def load_page1(s):
            tag = "page1_%d" % s if s < OWN_PAGES else staging(PAGE_BUFFERS[s - OWN_PAGES])
            tile = reuse.tile([P, T2], F32, name="page1_tile", tag=tag)
            nc.sync.dma_start(tile[:], page1[rows_of(s), :])
            return tile

        w1_raw, w3_raw, state_page, out_page = {}, {}, {}, {}
        idx = load_list("idx", offs)
        wgs_sb = load_rows("wgs_sb", wgs)
        table = [load_table(0)]
        vec_rows = keep.tile([P, P], F32, name="vec_rows")
        nc.gpsimd.memset(vec_rows[:], 0.0)
        for v, vec in enumerate((sens, gain, shift, back)):
            nc.scalar.dma_start(vec_rows[SLICES * v : SLICES * (v + 1), :], vec.rearrange("(s p) -> s p", p=P))
        ident = keep.tile([P, P], F32, name="ident")
        make_identity(nc, ident[:])
        table_scales = load_scale_rows("table_scales", tab_scales, T, nc.scalar)
        table = table + [load_table(1), load_table(2)]
        w2_sc = load_scale_rows("w2_sc", w2_scales, H, nc.sync)
        w2_parts = [load_w2(*W2_PARTS[0])]
        w1_raw[0] = load_w1(0)
        w1_raw[1] = load_w1(1)
        w2_parts.append(load_w2(*W2_PARTS[1]))
        idx2 = load_list("idx2", offs2)
        state_page[0] = load_page0(0)
        w1_raw[2] = load_w1(2)
        idx3 = load_list("idx3", offs3)
        for s in range(1, SLICES - 2):
            state_page[s] = load_page0(s)
            if s + 2 == W2_PARTS[2][0]:
                w2_parts.append(load_w2(*W2_PARTS[2]))
            w1_raw[s + 2] = load_w1(s + 2)

        v_words = keep.tile([P, PASSES_1, S], U32, name="v_words", align_bytes=64)
        v_scales = keep.tile([P, PASSES_1, S], U8, name="v_scales", align_bytes=64)
        for a in range(PASSES_1):
            nc.vector.tensor_copy(v_scales[:, a, :], table_scales[:, a * T : (a + 1) * T].indirect(idx[:]))
        for a in range(PASSES_1):
            nc.vector.tensor_copy(v_words[:, a, :], table[a][:].indirect(idx[:]))

        vec_ps = psum.tile([P, P], F32, name="vec_ps", tag="turn")
        nc.tensor.transpose(vec_ps[:], vec_rows[:], ident[:])
        vec_cols = keep.tile([P, 4 * SLICES], F32, name="vec_cols")
        nc.scalar.copy(vec_cols[:], vec_ps[:, 0 : 4 * SLICES])

        def column(v, s):
            return vec_cols[:, SLICES * v + s : SLICES * v + s + 1]

        def ahead_of(s):
            return s + 2 if s >= RAMP else s + 1

        work = [keep.tile([P, S + HALF], F32, name="work%d" % n) for n in range(SLICES + TURN_LAG)]
        z = [work[s][:, 0:S] for s in range(SLICES)]
        gain_wgs = [work[s + 2 if s > RAMP else s + 1][:, 0:S] for s in range(SLICES)]
        for s in range(SLICES):
            nc.scalar.activation(gain_wgs[s], wgs_sb[:], ACT.Copy, scale=column(GAIN, s))
        picked_first = [work[s + 1][:, 0:HALF] for s in range(SLICES)]
        x = [work[s + TURN_LAG][:, HALF : HALF + S] for s in range(SLICES)]
        x_codes = [keep.tile([P, S], U32, name="x_codes%d" % b, align_bytes=64) for b in range(PASSES_2)]
        x_scales = [keep.tile([P, S], U8, name="x_scales%d" % b, align_bytes=64) for b in range(PASSES_2)]
        w1_mx, w3_mx, pair_tiles, x_turned, turned_ps = {}, {}, {}, {}, {}

        def pair_tile(n):
            if n not in pair_tiles:
                buffer = n if n < SLICES else PASSES_2 * (n - SLICES) + 1
                pair_tiles[n] = reuse.tile([P, 2, S], F32, name="pair_tile", tag=staging(buffer))
            return pair_tiles[n]

        def quantise_w1(s):
            codes = reuse.tile([P, PASSES_1 * P], U32, name="w1_codes", tag="w1_codes", bufs=3, align_bytes=64)
            scales = reuse.tile([P, PASSES_1 * P], U8, name="w1_scales", tag="w1_scales", bufs=3, align_bytes=64)
            woven = reuse.tile([P, PASSES_1 * K_PASS], BF16, name="w1_woven", tag="woven", bufs=3, align_bytes=64)
            weave = nc.vector.tensor_copy if s == 1 else nc.scalar.copy
            for lo, hi in ((0, 1), (1, 2), (2, 3)) if s < 2 else ((0, 2), (2, 3)):
                part = woven[:, lo * K_PASS : hi * K_PASS]
                weave(
                    part.rearrange("p (a c i t) -> p a c t i", a=hi - lo, i=LINE, t=PACK),
                    w1_raw[s][:, lo:hi, :, :].rearrange("p a t (c i) -> p a c t i", i=LINE),
                )
                cols = slice(lo * P, hi * P)
                nc.vector.quantize_mx(out=codes[:, cols].bitcast(FP8X4), scales=scales[:, cols], in_=part)
            w1_mx[s] = codes, scales

        def quantise_w3(piece):
            shape = [P, PIECE_WIDTH * PACK]
            if piece < PIECES_BEFORE:
                woven = reuse.tile(shape, BF16, name="w3_woven", tag="woven", bufs=3, align_bytes=64)
            else:
                tag = ("x_turned11", "x_woven11")[piece % 2]
                woven = reuse.tile(shape, BF16, name="w3_woven", tag=tag, align_bytes=64)
            nc.scalar.copy(
                woven[:].rearrange("p (c i t) -> p c t i", i=LINE, t=PACK),
                w3_raw[piece][:].rearrange("p t (c i) -> p c t i", i=LINE),
            )
            codes = keep.tile([P, PIECE_WIDTH], U32, name="w3_codes%d" % piece, align_bytes=64)
            scales = keep.tile([P, PIECE_WIDTH], U8, name="w3_scales%d" % piece, align_bytes=64)
            nc.vector.quantize_mx(out=codes[:].bitcast(FP8X4), scales=scales[:], in_=woven[:])
            w3_mx[piece] = codes, scales

        def first_products(s):
            a_ps = psum.tile([P, S], F32, name="a_ps", tag="sum_a")
            b_ps = psum.tile([P, S], F32, name="b_ps", tag="sum_b")
            part = [lo <= s < hi for lo, hi in W2_PARTS].index(True)
            w2_byte = 2 * P * (s - W2_PARTS[part][0])
            codes, scales = w1_mx[s]
            for a in range(PASSES_1):
                nc.tensor.matmul_mx(
                    out=b_ps[:],
                    lhsT=w2_parts[part][:, a, w2_byte : w2_byte + 2 * P].bitcast(FP4X4),
                    lhsT_scale=w2_sc[:, a * H + s * P : a * H + (s + 1) * P],
                    rhs=v_words[:, a, :].bitcast(FP8X4), rhs_scale=v_scales[:, a, :],
                    start=(a == 0), stop=(a == PASSES_1 - 1),
                )
            for a in range(PASSES_1):
                cols = slice(a * P, (a + 1) * P)
                nc.tensor.matmul_mx(
                    out=a_ps[:], lhsT=codes[:, cols].bitcast(FP8X4), lhsT_scale=scales[:, cols],
                    rhs=v_words[:, a, :].bitcast(FP8X4), rhs_scale=v_scales[:, a, :],
                    start=(a == 0), stop=(a == PASSES_1 - 1),
                )
            b_sb = pair_tile(s)[:, 0, :]
            nc.scalar.copy(b_sb, b_ps[:])
            nc.vector.scalar_tensor_tensor(z[s], a_ps[:], column(SENS, s), b_sb, ALU.mult, ALU.add)

        def put_state(s):
            tanh_z = pair_tile(ahead_of(s) if s > 0 else 0)[:, 1, :]
            nc.scalar.activation(tanh_z, z[s], ACT.Tanh)
            nc.vector.tensor_tensor(state_page[s][:].indirect(idx2[:]), tanh_z, gain_wgs[s], ALU.mult)

        def recall(s, half, picked):
            offsets = idx3[:, half * HALF // GROUP : (half + 1) * HALF // GROUP]
            nc.vector.tensor_copy(picked, state_page[s][:].indirect(offsets))

        def add_shift(s, half, picked):
            x_half = x[s][:, half * HALF : (half + 1) * HALF]
            nc.scalar.activation(x_half, picked, ACT.Identity, bias=column(SHIFT, s))

        def turn(s, half):
            b, q = divmod(s, SLICES_PER_PASS)
            if q % 2 == 0:
                turned_ps[half] = psum.tile([P, 2, 2, P], F32, name="turned_ps", tag="turn")
            for c in range(2):
                first = half * HALF + c * P
                nc.tensor.transpose(turned_ps[half][:, c, q % 2, :], x[s][:, first : first + P], ident[:])
            if q == 0:
                x_turned[half, b] = reuse.tile(
                    [P, 2, 2, SLICES_PER_PASS, 32, 2], BF16, name="x_turned%d%d" % (half, b), align_bytes=64
                )
            if q % 2 == 1:
                nc.scalar.copy(
                    x_turned[half, b][:, :, :, q - 1 : q + 1, :, :].rearrange("j c u q m e -> j c u (q m) e"),
                    turned_ps[half][:].rearrange("j c q (m u e) -> j c u (q m) e", u=2, e=2),
                )
            if q == SLICES_PER_PASS - 1:
                quantise_x(half, b)

        def quantise_x(half, b):
            words = x_turned[half, b][:].rearrange("j c u q m e -> j (c u q m e)").bitcast(F32)
            tag = "x_woven_pass0" if b == 0 else "x_woven%d1" % half
            woven = reuse.tile([P, HALF * PACK], BF16, name="x_woven", tag=tag, align_bytes=64)
            back_ps = psum.tile([P, 2, 2, P], F32, name="back_ps", tag="turn_back")
            for c in range(2):
                for u in range(2):
                    first = (c * 2 + u) * P
                    nc.tensor.transpose(back_ps[:, c, u, :], words[:, first : first + P], ident[:])
            nc.scalar.copy(
                woven[:].bitcast(F32).rearrange("p (c j u) -> p c j u", c=2, u=2),
                back_ps[:].rearrange("p c u j -> p c j u"),
            )
            cols = slice(half * HALF, (half + 1) * HALF)
            nc.vector.quantize_mx(out=x_codes[b][:, cols].bitcast(FP8X4), scales=x_scales[b][:, cols], in_=woven[:])

        def last_product(s, lo, hi, y):
            e_ps = psum.tile([P, hi - lo], F32, name="e_ps", tag=("sum_a", "sum_b")[s % 2])
            cols = slice((s % 2) * P, (s % 2 + 1) * P)
            for b in reversed(range(PASSES_2)):
                codes, scales = w3_mx[PASSES_2 * (s // 2) + b]
                nc.tensor.matmul_mx(
                    out=e_ps[:], lhsT=codes[:, cols].bitcast(FP8X4), lhsT_scale=scales[:, cols],
                    rhs=x_codes[b][:, lo:hi].bitcast(FP8X4), rhs_scale=x_scales[b][:, lo:hi],
                    start=(b == PASSES_2 - 1), stop=(b == 0),
                )
            nc.vector.scalar_tensor_tensor(y, x[s][:, lo:hi], column(BACK, s), e_ps[:], ALU.mult, ALU.max)

        def put_features(s, lo, hi, y):
            offsets = idx4[:, lo // GROUP : hi // GROUP]
            nc.vector.tensor_tensor(out_page[s][:].indirect(offsets), y, wgo_sb[:, lo:hi], ALU.mult)
            if hi == S:
                nc.sync.dma_start(out[rows_of(s), :], out_page[s][:])

        quantise_w1(0)
        first_products(0)
        multiplied = 0
        for s in range(SLICES):
            for n in range(ahead_of(s - 1) + 1, ahead_of(s) + 1):
                if n < SLICES:
                    quantise_w1(n)
                else:
                    for piece in range(PASSES_2 * (n - SLICES), PASSES_2 * (n - SLICES + 1)):
                        w3_raw[piece] = load_w3(piece)
                        quantise_w3(piece)
                    state_page[s] = load_page0(s)
            put_state(s)
            if s > 0:
                recall(s - 1, 0, picked_first[s - 1])
            for n in range(multiplied + 1, min(ahead_of(s), SLICES - 1) + 1):
                first_products(n)
                multiplied = n
            if s >= TURN_LAG:
                add_shift(s - TURN_LAG, 0, picked_first[s - TURN_LAG])
                turn(s - TURN_LAG, 0)

        wgo_sb = load_rows("wgo_sb", wgo)
        idx4 = load_list("idx4", offs4)
        for s in range(EARLY):
            out_page[s] = load_page1(s)
        for piece in range(PIECES_BEFORE, PIECES):
            w3_raw[piece] = load_w3(piece)
        for s in range(EARLY, SLICES - 2):
            out_page[s] = load_page1(s)

        for s in range(SLICES - TURN_LAG, SLICES):
            if s == SLICES - 2:
                recall(SLICES - 1, 0, picked_first[SLICES - 1])
            add_shift(s, 0, picked_first[s])
            turn(s, 0)
        for s in range(EARLY - 1):
            last_product(s, 0, HALF, x[s][:, 0:HALF])

        picked_a = reuse.tile([P, LATE_SPLIT, HALF], F32, name="picked_a", tag=staging(PIECES_BEFORE - 1))
        picked_b = reuse.tile([P, SLICES - LATE_SPLIT, HALF], F32, name="picked_b", tag="x_woven01", align_bytes=64)
        for s in range(SLICES):
            picked = picked_a[:, s, :] if s < LATE_SPLIT else picked_b[:, s - LATE_SPLIT, :]
            recall(s, 1, picked)
            add_shift(s, 1, picked)
        for s in range(SLICES):
            turn(s, 1)
        for s in range(EARLY - 1):
            put_features(s, 0, HALF, x[s][:, 0:HALF])
        y_after = reuse.tile([P, HALF], F32, name="y_after", tag="x_woven11", align_bytes=64)
        last_product(EARLY - 1, 0, HALF, y_after[:])
        put_features(EARLY - 1, 0, HALF, y_after[:])
        for piece in range(PIECES_BEFORE, PIECES):
            quantise_w3(piece)
        for s in range(SLICES - 2, SLICES):
            out_page[s] = load_page1(s)

        first_entry = [HALF if s < EARLY else 0 for s in range(SLICES)]
        last_product(0, first_entry[0], S, x[0][:, first_entry[0] : S])
        for s in range(SLICES):
            if s + 1 < SLICES:
                last_product(s + 1, first_entry[s + 1], S, x[s + 1][:, first_entry[s + 1] : S])
            put_features(s, first_entry[s], S, x[s][:, first_entry[s] : S])
